import numpy as np, ml_dtypes
CORES = [25,29,65,69,153,157,193,197]
N = 8
BF = ml_dtypes.bfloat16
def gentries(a):
    return np.ascontiguousarray(a.reshape(8, 16, -1).transpose(0, 2, 1)).reshape(8, -1)
def gtable(e):
    e = np.asarray(e); return np.ascontiguousarray(e.reshape(8, -1, 16).transpose(0, 2, 1)).reshape(128, -1).astype(np.int32)
NL, H, L, K, S, RO = 2048, 1024, 64, 16, 3, 5
MT = [12, 18, 14, 22, 16]
AT = [10, 8, 9, 6, 8]
def own(rng, c):
    return np.take_along_axis(c, rng.integers(0, K, (N, 8, 1, L)), 2)[:, :, 0]
def parts(rng):
    v = rng.integers(0, 256, (N, 8, 16, NL))
    g = 2 * np.argsort(rng.random((N, 8, 16, H)), axis=-1) + rng.integers(0, 2, (N, 8, 16, H))
    c = rng.integers(0, NL, (N, 8, K, L)); d = rng.integers(0, NL, (N, 8, K, L))
    return v, g, c, d, own(rng, c)
def pack(v, g, c, d, l):
    return {"val": np.ascontiguousarray(v.reshape(N, 128, NL)).astype(np.float32).astype(BF), "gen": np.ascontiguousarray(g.reshape(N, 128, H)).astype(np.int32),
            "cla": np.stack([gtable(a.reshape(8, -1)) for a in c]), "par": np.stack([gtable(a.reshape(8, -1)) for a in d]), "lit": np.stack([gtable(a) for a in l])}
def setup_inputs(rng):
    return pack(*parts(rng))
def setup_inputs_corners(rng):
    v, g, c, d, l = parts(rng)
    top = rng.random((N, 8, 1, NL)) < 1.0 / K
    v = np.where(top, rng.choice(np.array([222, 223, 224, 240, 255]), v.shape), rng.choice(np.array([0, 1, 31, 32, 33, 100]), v.shape))
    v[0, 6] = 0; v[1, 6] = 255
    g[:, 0, 3] = 2 * np.arange(H); g[:, 0, 15] = 2 * np.arange(H) + 1
    g[:, 1] = g[:, 1, :1].copy(); g[:, 2, ::4] = 0; g[:, 2, 1::4] = NL - 1
    c[..., 0::5] = d[..., 0::5]
    c[..., 1::5] = c[:, :, :1, 1::5].copy()
    c[:, :, 1::2, 2::5] = c[:, :, 0::2, 2::5] ^ 1
    e = c[..., 3::5]; c[..., 3::5] = rng.choice(np.array([0, 1, NL - 2, NL - 1]), e.shape)
    l[..., 0::3] = 0; l[..., 1::3] = NL - 1; l[..., 2::3] = c[:, :, K - 1, 2::3]
    return pack(v, g, c, d, l)
def setup_inputs_crowd(rng):
    v, g, c, d, l = parts(rng)
    for q in range(N):
        for s in range(8):
            w = 2 * rng.permutation(H)[:2 * K] + rng.integers(0, 2, 2 * K); c[q, s] = w[:K, None]; d[q, s] = w[K:, None]
            j = 15 if s == 7 else int(rng.integers(0, 16)); k = K - 1 if s == 0 else int(rng.integers(0, K))
            im = g[q, s, j, w[:K] >> 1] ^ (w[:K] & 1); both = np.concatenate([im, im ^ 1])
            v[q, s][:, both] = np.minimum(v[q, s][:, both], 100); v[q, s][:, im[k]] = 255; l[q, s] = im[k]
            if s in (2, 5):
                turn = rng.random(L) < 0.5; c[q, s] = np.where(turn, c[q, s] ^ 1, c[q, s]); v[q, s][:, im[k] ^ 1] = 255
            if s & 1:
                o = 0 if s == 1 else L - 1 if s == 7 else int(rng.integers(0, L))
                c[q, s, :, o] = int(c[q, s, 0, o]); d[q, s, :, o] = int(d[q, s, 0, o])
    return pack(v, g, c, d, l)
def endclauses(rng):
    E = np.array([0, NL - 1]); sh = (N, 8, 1, L); b = rng.integers(0, 2, sh); x = E[b]; y = E[1 - b]; kind = rng.integers(0, 4, sh)
    k1 = rng.integers(0, K, sh); k2 = (k1 + rng.integers(1, K, sh)) % K; k = np.arange(K).reshape(1, 1, K, 1)
    c = np.where(k == k1, y, x); c = np.where((kind == 2) & (k == k2), x ^ 1, c)
    return np.where(kind == 3, E[rng.integers(0, 2, (N, 8, K, L))], c)
def setup_inputs_ends(rng):
    E = np.array([0, NL - 1]); v = 255 * rng.integers(0, 2, (N, 8, 16, NL)); g = E[rng.integers(0, 2, (N, 8, 16, H))]
    c = endclauses(rng); d = endclauses(rng); l = E[rng.integers(0, 2, (N, 8, L))]
    for o, k in ((0, 0), (L - 1, K - 1)):
        c[:, :, :, o] = NL - 1; c[:, :, k, o] = 0
    h = (np.arange(16) < 8).astype(np.int64); on = np.ones(16, np.int64); no = 0 * on
    for q in range(N):
        for s in range(8):
            ty = (3 * q + s) % 6
            if q == N - 1 and s == 7: ty = 0
            if q in (0, 2) and s == 6: ty = 6
            four = [[on, no, no, on], [no, on, on, no], [h, no, no, 1 - h], [no, h, 1 - h, no], list(rng.integers(0, 2, (4, 16))), [on, no, no, on], [on, no, no, no]][ty]
            four = np.stack(four)
            if ty == 5: four[:, 13:] = rng.integers(0, 2, (4, 3))
            if ty == 6: g[q, s, :2, 0] = NL - 1; g[q, s, 2:, 0] = 0
            v[q, s][:, [0, 1, NL - 2, NL - 1]] = 255 * four.T
    return pack(v, g, c, d, l)
def setup_inputs_spread(rng):
    v, g, c, d, l = parts(rng)
    v = np.minimum((1.1 * np.exp2(8 * rng.random((N, 8, 1, NL))) * rng.random((N, 8, 16, NL))).astype(np.int64), 255)
    v[:, 1::2] = np.minimum((256 * rng.random((N, 4, 16, NL)) ** np.exp2(rng.integers(-1, 3, (N, 4, 16, 1)))).astype(np.int64), 255)
    g[:, :, ::2] = 2 * np.minimum((H * rng.random((N, 8, 8, H)) ** 3).astype(np.int64), H - 1) + rng.integers(0, 2, (N, 8, 8, H))
    p = rng.choice(np.array([1, 2, 4]), (N, 8, 1, 1))
    c = np.minimum((NL * rng.random((N, 8, K, L)) ** p).astype(np.int64), NL - 1); d = NL - 1 - np.minimum((NL * rng.random((N, 8, K, L)) ** p).astype(np.int64), NL - 1)
    l = np.where(rng.random((N, 8, L)) < 0.5, own(rng, c), own(rng, d))
    return pack(v, g, c, d, l)
def apart(rng, v, g, c, d, l, s, one):
    w = rng.permutation(H); z = 2 * w[:L] + rng.integers(0, 2, L); r = w[L:]; m = np.zeros(H, np.int64)
    m[z >> 1] = np.roll(z, -1) ^ (z & 1); m[r] = 2 * rng.permutation(r) + rng.integers(0, 2, H - L); g[:, s, 0] = m
    v[:, s] = np.minimum(v[:, s], 100); v[:, s][:, :, z] = 255; v[:, s][:, :, z ^ 1] = rng.integers(200, 256, (N, 16, L))
    c[:, s] = 2 * r[rng.integers(0, H - L, (N, K, L))] + rng.integers(0, 2, (N, K, L))
    for q in range(N):
        y = rng.permutation(z); c[q, s, rng.integers(0, K, L), np.arange(L)] = y; l[q, s] = y
        if one:
            o = L - 1 if q == N - 1 else int(rng.integers(0, L))
            c[q, s, :, o] = int(c[q, s, 0, o]); d[q, s, :, o] = int(d[q, s, 0, o])
def setup_inputs_ties(rng):
    v, g, c, d, l = parts(rng); m = np.array(MT)[np.arange(8) % RO].reshape(1, 8, 1, 1); u = K * rng.random((N, 8, 1, NL))
    low = (rng.random(v.shape) * (255 - m)).astype(np.int64)
    w = np.where(u < 1, 255, np.where(u < 1.3, 255 - m, np.where(u < 4, 254 - m, low)))
    v = np.where(rng.random(v.shape) < 0.02, v, w)
    h = (np.arange(16) < 8).astype(np.int64).reshape(16, 1); x = u[:, [2, 5]]
    v[:, [2, 5]] = np.where(x < 1, 255 * h, np.where(x < 2, 255 * (1 - h), np.minimum(low[:, [2, 5]], 100)))
    eq = rng.random((N, 8, 1, H)) < 0.25; v[..., 1::2] = np.where(eq, v[..., 0::2], v[..., 1::2])
    apart(rng, v, g, c, d, l, 6, False); apart(rng, v, g, c, d, l, 7, True)
    return pack(v, g, c, d, l)
def check_inputs(d):
    bad = []
    for k, lo, hi in (("val", 0, 255), ("gen", 0, NL - 1), ("cla", 0, NL - 1), ("par", 0, NL - 1), ("lit", 0, NL - 1)):
        a = np.asarray(d[k]).astype(np.float64)
        if not (np.min(a) >= lo and np.max(a) <= hi): bad.append("range of " + k)
        elif np.any(a != np.floor(a)): bad.append("whole numbers of " + k)
    return bad
def reference(val, gen, cla, par, lit):
    V = val.astype(np.float32).astype(np.int16).reshape(N, 8, 16, NL)
    e = gen.astype(np.int64).reshape(N, 8, 16, H); P = np.stack([e, e ^ 1], axis=-1).reshape(N, 8, 16, NL)
    C = np.stack([gentries(a) for a in cla]).astype(np.int64).reshape(N, 8, K, L); D = np.stack([gentries(a) for a in par]).astype(np.int64).reshape(N, 8, K, L)
    l = np.stack([gentries(a) for a in lit]).astype(np.int64); A = np.zeros((N, 8), np.int64)
    for t in range(RO):
        if t: C = np.roll(C, S, axis=0); D = np.roll(D, S, axis=0); l = np.roll(l, S, axis=0)
        for a in range(N):
            v = V[a]; x = l[a][:, None, :]
            less = np.take_along_axis(v, x, 2) < np.take_along_axis(v, x ^ 1, 2)
            c = np.where((np.add.reduce(less.astype(np.int64), axis=1) >= 9)[:, None, :], D[a], C[a])
            img = np.take_along_axis(P[a], c.reshape(8, 1, K * L), 2)
            w = np.take_along_axis(v, img.reshape(8, 1, 16 * K * L), 2).reshape(8, 16, 16, K, L)
            near = w >= np.max(w, axis=3)[:, :, :, None] - MT[t]
            unit = np.add.reduce(near, axis=3, dtype=np.int16) == 1
            votes = np.add.reduce(unit.astype(np.int64), axis=1); js = np.argmax(votes, axis=1)
            pro = np.max(votes, axis=1) >= (AT[t] + (A[a] & 1))[:, None]
            new = np.take_along_axis(img.reshape(8, 16, K, L), js[:, None, None, :], 1)[:, 0]
            un = np.take_along_axis(unit, js[:, None, None, :], 2)[:, :, 0]
            vn = np.take_along_axis(v, new.reshape(8, 1, K * L), 2).reshape(8, 16, K, L).astype(np.int64)
            ks = np.argmax(np.add.reduce(np.where(un[:, :, None, :], vn, 0), axis=1), axis=1)
            nl = np.take_along_axis(new, ks[:, None, :], 1)[:, 0]
            C[a] = np.where(pro[:, None, :], new, D[a]); D[a] = c; l[a] = np.where(pro, nl, l[a])
            for g in range(8):
                z = nl[g, np.flatnonzero(pro[g])]
                z = z[np.unique(z >> 1, return_index=True)[1]]
                up = np.minimum(v[g][:, z] + 32, 255); down = np.maximum(v[g][:, z ^ 1] - 32, 0)
                v[g][:, z] = up; v[g][:, z ^ 1] = down
            A[a] = np.add.reduce(pro.astype(np.int64), axis=1)
    return {"yv": V.reshape(N, 128, NL).astype(np.float32).astype(BF), "yc": np.stack([gtable(a.reshape(8, -1)) for a in C]).astype(np.float32),
            "yd": np.stack([gtable(a.reshape(8, -1)) for a in D]).astype(np.float32), "yl": np.stack([gtable(a) for a in l]).astype(np.float32)}

@@ -1,0 +1,540 @@
+from concourse.mybir import dt, AluOpType, AxisListType, ActivationFunctionType
+
+A_ = AluOpType
+F = ActivationFunctionType
+X_ = AxisListType.X
+NR_ = 5
+BAT = {"A": (0, 32), "B": (32, 32)}
+NV = 8
+PRE = 8
+MAGIC = 12582912.0
+
+_SIZE = {"float32": 4, "int32": 4, "uint16": 2, "float16": 2, "bfloat16": 2}
+SCRATCH = {}
+for _d, _names in (("int32", "GEN 1024 CW0 64 CW 64 PI 8 XC 64 XD 64 XL 4 LT0 4 LT1 4 TI 2"),
+                   ("float32", "GM 1024 PM 1024 PT 2048 K1 1024 K2 1024 B64 64 PENC 64 LMT 192 PC 16 DC 64 Z 128 ZT 128 Z2 128 ZT2 128 "
+                               "YC 64 YD 64 YL 4 PREP 64 PRO 64 THR 4"),
+                   ("bfloat16", "VAL 2176 W 16384 U 1024 UX 1024 PR 1024 MSK 256 MKK 512 ONE 128 BO 128 B1 128 BOV 128 BOS 128 IDN 128 "
+                                "E0 128 SL0 2048 JT 512 A16 512 OHT 512"),
+                   ("float16", "IMF 1024 MK 1024 BOH 128 IDH 128 SEL 2048"), ("uint16", "IMG 1024")):
+    _w = _names.split()
+    for _i in range(0, len(_w), 2):
+        SCRATCH[_w[_i]] = ("sbuf", [128, int(_w[_i + 1])], _d)
+for _i in (0, 1):
+    SCRATCH["SB%d" % _i] = ("sbuf", [128, 257, 16], "bfloat16")
+    SCRATCH["YB%d" % _i] = ("sbuf", [128, 256, 16], "bfloat16")
+for _n in "psD0 psD1 psV0 psV1 psS psN psR".split():
+    SCRATCH[_n] = ("psum", [128, 512], "float32")
+SEMAPHORES = "vc sc tc gc ls ld0 ld1 ld2 ld3 ld4 st0 st1 st2 st3".split()
+_POS = {}
+
+
+def _declare():
+    tot = {}
+    for b, (a0, n) in BAT.items():
+        nq = n // 16
+        for t in range(NR_):
+            SCRATCH["i%s%d" % (b, t)] = ("sbuf", [128, 2 * n + 2 * nq], "float16")
+            SCRATCH["o%s%d" % (b, t)] = ("sbuf", [128, 2 * n + 2 * nq], "float16")
+            if t:
+                SEMAPHORES.append("a%s%d" % (b, t))
+        for d, names in (("uint16", (("LL", 2 * nq), ("CU", n), ("LU", n), ("LW", n), ("EL", 2 * nq))),
+                         ("bfloat16", (("XV", 2 * n), ("LE", n), ("ZE", 2 * n))),
+                         ("int32", (("KI", n), ("QI", n), ("WI", n), ("K2I", n), ("KR", n))),
+                         ("float16", (("PEN", n), ("NCG", n), ("XX", n))),
+                         ("float32", (("DMC", n), ("FL", n), ("T2", n), ("NP", n), ("DN", n), ("OHK", n), ("DM", n), ("NL", 2 * nq),
+                                      ("PCL", nq), ("EQ", 64 * nq), ("EM", 64 * nq), ("DV", 2 * nq), ("FP", nq), ("LP", nq),
+                                      ("OL", 2 * nq), ("YE", 2 * n), ("KP", 2 * nq), ("DL", 2 * nq), ("DK", 2 * nq)))):
+            for nm, w in names:
+                al = 64 // _SIZE[d]
+                _POS[nm + b] = ("pk_" + d, tot.get(d, 0), w)
+                tot[d] = tot.get(d, 0) + (w + al - 1) // al * al
+    for d in tot:
+        SCRATCH["pk_" + d] = ("sbuf", [128, tot[d]], d)
+
+
+_declare()
+
+
+def _route(r, T, topo):
+    s, d = T.cores[r], T.cores[(r + 3) % len(T.cores)]
+    if topo.may_write(s, d):
+        return s, None, d
+    own = [c for c in topo.cores_of(s) if c not in T.cores and topo.may_write(c, d)]
+    own.sort(key=lambda c: (topo.die(c) != topo.die(s), c))
+    return s, own[0], d
+
+
+def _mask(src, dst, topo):
+    e = topo.engines(src, dst)[:8]
+    return sum(1 << x for x in e), len(e)
+
+
+def _send(g, T, topo, core, dst, src_ap, name, sem):
+    rid, pid = topo.addr(dst, core)
+    m, k = _mask(core, dst, topo)
+    g.remote_dma(T[name][:], src_ap, T.sem[sem], T.sem["ls"], pid, rid, m)
+    return k
+
+
+def _relay(g, core, T, topo):
+    for r in range(len(T.cores)):
+        s, h, d = _route(r, T, topo)
+        if h != core:
+            continue
+        tot = 0
+        for t in range(1, NR_):
+            for b in BAT:
+                nm, sem = "i%s%d" % (b, t), "a%s%d" % (b, t)
+                g.wait_ge(T.sem[sem], _mask(s, h, topo)[1])
+                tot += _send(g, T, topo, core, d, T[nm][:], nm, sem)
+        g.wait_ge(T.sem["ls"], tot)
+
+
+def rank_program(g, core, T, topo):
+    rank = T.rank_of(core)
+    if rank is None:
+        return _relay(g, core, T, topo)
+    MT, AT = (12, 18, 14, 22, 16), (10, 8, 9, 6, 8)
+    eng = {"v": g.vector, "s": g.scalar, "t": g.tensor, "g": g, "y": g.sync}
+    cnt, total, hist = {}, {}, {}
+    known = {q: {} for q in eng}
+    V, S, TE = g.vector, g.scalar, g.tensor
+
+    def need(q, reads, writes):
+        w = {}
+        for keys, wr in ((reads, False), (writes, True)):
+            for (key, c0, c1) in keys:
+                for h in hist.get(key, ()):
+                    if h[0] >= c1 or c0 >= h[1] or h[3] == q == "t":
+                        continue
+                    if not (wr or h[2] or (key[:2] == "ps" and h[3] != q)):
+                        continue
+                    s, n = h[4]
+                    w[s] = max(w.get(s, 0), n)
+        for s in w:
+            if known[q].get(s, 0) < w[s]:
+                eng[q].wait_ge(T.sem[s], w[s])
+                known[q][s] = w[s]
+
+    def note(q, reads, writes, ev):
+        for keys, wr in ((reads, False), (writes, True)):
+            for (key, c0, c1) in keys:
+                L = hist.setdefault(key, [])
+                if wr:
+                    L[:] = [h for h in L if not (c0 <= h[0] and h[1] <= c1)]
+                else:
+                    L[:] = [h for h in L if h[2] or h[3] != q or not (c0 <= h[0] and h[1] <= c1)]
+                L.append((c0, c1, wr, q, ev))
+
+    def op(q, fn, reads, writes):
+        need(q, reads, writes)
+        sem = q + "c"
+        total[sem] = cnt[q] = cnt.get(q, 0) + 1
+        fn().then_inc(T.sem[sem], 1)
+        note(q, reads, writes, (sem, cnt[q]))
+
+    def dma(q, o, i, reads, writes, sem):
+        need(q, reads, writes)
+        eng[q].dma_start(o, i).then_inc(T.sem[sem], 16)
+        total[sem] = 16
+        note("dma" + sem, reads, writes, (sem, 16))
+
+    def B(name, c0=0, c1=None, st=1):
+        base, off, w = _POS[name] if name in _POS else (name, 0, SCRATCH[name][1][1])
+        c1 = w if c1 is None else c1
+        ap = T[base][:, off + c0:off + c1] if st == 1 else T[base][:, off + c0:off + c1:st]
+        return ap, ((base, 0, 512) if base[:2] == "ps" else (base, off + c0, off + c1))
+
+    def vcopy(o, i):
+        op("v", lambda: V.tensor_copy(o[0], i[0]), [i[1]], [o[1]])
+
+    def vgat(o, win, off):
+        op("v", lambda: V.tensor_copy(o[0], win[0].indirect(off[0])), [win[1], off[1]], [o[1]])
+
+    def sgat(o, win, off):
+        op("s", lambda: S.activation(o[0], win[0].indirect(off[0]), F.Copy), [win[1], off[1]], [o[1]])
+
+    def act(o, i, scale, bias, f=F.Copy):
+        op("s", lambda: S.activation(o[0], i[0], f, bias=bias, scale=scale), [i[1]], [o[1]])
+
+    def tt(o, a, b, f):
+        op("v", lambda: V.tensor_tensor(o[0], a[0], b[0], f), [a[1], b[1]], [o[1]])
+
+    def ttg(o, win, off, b, f):
+        op("v", lambda: V.tensor_tensor(o[0], win[0].indirect(off[0]), b[0], f), [win[1], off[1], b[1]], [o[1]])
+
+    def ts(o, a, s1, f1, s2=None, f2=None):
+        rd = [a[1]] + [s[1] for s in (s1, s2) if isinstance(s, tuple)]
+        x1 = s1[0] if isinstance(s1, tuple) else s1
+        x2 = s2[0] if isinstance(s2, tuple) else s2
+        if f2 is None:
+            op("v", lambda: V.tensor_scalar(o[0], a[0], x1, None, f1), rd, [o[1]])
+        else:
+            op("v", lambda: V.tensor_scalar(o[0], a[0], x1, x2, f1, f2), rd, [o[1]])
+
+    def red(o, a, f):
+        op("v", lambda: V.tensor_reduce(o[0], a[0], X_, f), [a[1]], [o[1]])
+
+    def ms(o, c):
+        op("v", lambda: V.memset(o[0], c), [], [o[1]])
+
+    def mm(o, l, r, st, sp):
+        op("t", lambda: TE.matmul(o[0], l[0], r[0], st, sp), [l[1], r[1]], [o[1]])
+
+    def iota(o, pat, base, ch, whole=False):
+        if whole:
+            op("g", lambda: g.iota(o[0], pat, base, ch), [], [o[1]])
+        else:
+            op("g", lambda: g.iota(o[0], pat, base, ch, allow_small_or_imprecise_dtypes=True), [], [o[1]])
+
+    def asel(o, i, pat, f, base, ch):
+        op("g", lambda: g.affine_select(o[0], i[0], pat, f, 0.0, base, ch), [i[1]], [o[1]])
+
+    for q, nm, c1, src, sem in (("s", "GEN", 1024, T.gen, "ld3"), ("y", "XC", 64, T.cla, "ld0"), ("y", "XD", 64, T.par, "ld1"),
+                                ("y", "XL", 4, T.lit, "ld2"), ("y", "VAL", 2048, T.val, "ld4")):
+        o = B(nm, 0, c1)
+        dma(q, o[0], src[:], [], [o[1]], sem)
+
+    iota(B("PI", 0, 1), [[1, 1]], 0, 1, True)
+    ms(B("ONE"), 1.0)
+    ms(B("SL0"), 1.0)
+    for p in (0, 1):
+        op("v", lambda p=p: V.memset(T["SB%d" % p][:, 0, :], 0.0), [], [("SB%d.%d" % (p, j), 0, 1) for j in range(16)])
+    ms(B("MSK"), 1.0)
+    ms(B("MKK"), 1.0)
+    ms(B("VAL", 2048, 2176), 0.0)
+    ms(B("MSK", 15, 256, 16), -1.0)
+    ms(B("MKK", 0, 512, 16), 0.0)
+    ms(B("DC", 0, 32), 32.0)
+    ms(B("DC", 32, 64), -32.0)
+    ts(B("PI", 1, 2), B("PI", 0, 1), 15, A_.bitwise_and)
+    ts(B("PI", 2, 3), B("PI", 0, 1), 16, A_.bitwise_and)
+    vcopy(B("PC", 0, 1), B("PI", 1, 2))
+    ts(B("PC", 1, 2), B("PI", 2, 3), 0.0, A_.is_equal)
+    ts(B("PC", 2, 3), B("PI", 2, 3), 16.0, A_.is_equal)
+    ts(B("PC", 3, 4), B("PC", 0, 1), 16.0, A_.mult)
+    for q in range(4):
+        ts(B("PC", 4 + q, 5 + q), B("PC", 0, 1), 16.0 * q, A_.add)
+    for q in range(4):
+        ts(B("PC", 8 + q, 9 + q), B("PC", 4 + q, 5 + q), 2.0, A_.mult, 2048.0, A_.add)
+    ms(B("THR", 0, 1), -1024.0 * (AT[0] - 1))
+    asel(B("B1"), B("ONE"), [[-16, 8], [0, 16]], A_.is_ge, 0, 1)
+    asel(B("BO"), B("B1"), [[16, 8], [0, 16]], A_.is_ge, 15, -1)
+    asel(B("IDN"), B("ONE"), [[-1, 128]], A_.is_equal, 0, 1)
+    asel(B("E0"), B("ONE"), [[0, 128]], A_.is_equal, 0, 1)
+    iota(B("JT"), [[0, 32], [1, 16]], 0, 0)
+    iota(B("A16"), [[16, 32], [0, 16]], 0, 0)
+    iota(B("CW0"), [[240, 64]], 0, 0, True)
+    iota(B("B64"), [[1, 64]], 0, 0)
+    iota(B("PENC"), [[2, 64]], 2048, 0)
+    asel(B("SL0"), B("SL0"), [[1, 16], [0, 8], [-1, 16]], A_.is_equal, 0, 0)
+    asel(B("SL0"), B("SL0"), [[0, 16], [-16, 8], [0, 16]], A_.is_ge, 0, 1)
+    asel(B("SL0"), B("SL0"), [[0, 16], [16, 8], [0, 16]], A_.is_ge, 15, -1)
+
+    def flip(Z, ZT, src, dst):
+        for q in range(4):
+            for h in range(2):
+                ts(B(Z, 32 * q + 16 * h, 32 * q + 16 * h + 16), src(q), B("PC", 1 + h, 2 + h), A_.mult)
+        a, b = B(Z), B(ZT)
+        op("v", lambda: V.transpose(b[0], a[0]), [a[1]], [b[1]])
+        for q in range(4):
+            tt(dst(q), B(ZT, 32 * q, 32 * q + 16), B(ZT, 32 * q + 16, 32 * q + 32), A_.add)
+
+    def lane16(pre, t, part):
+        def f(q):
+            b = "A" if 16 * q < BAT["B"][0] else "B"
+            c = part * BAT[b][1] + 16 * q - BAT[b][0]
+            return B("%s%s%d" % (pre, b, t), c, c + 16)
+        return f
+
+    flip("Z", "ZT", lambda q: B("XC", q, 64, 4), lane16("i", 0, 0))
+    HF = ((0, 512), (512, 1024))
+    for c0, c1 in HF:
+        vcopy(B("PT", 2 * c0, 2 * c1, 2), B("GEN", c0, c1))
+    for i, (c0, c1) in enumerate(HF):
+        act(B("PM", c0, c1), B("PT", 2 * c0, 2 * c1, 2), 0.49994, MAGIC)
+        act(B("psD%d" % i), B("PM", c0, c1), 4.0, -4.0 * MAGIC)
+    for c0, c1 in HF:
+        ts(B("GM", c0, c1), B("GEN", c0, c1), 1.0, A_.subtract)
+    flip("Z2", "ZT2", lambda q: B("XD", q, 64, 4), lane16("i", 0, 1))
+    for i, (c0, c1) in enumerate(HF):
+        tt(B("PT", 2 * c0 + 1, 2 * c1, 2), B("psD%d" % i), B("GM", c0, c1), A_.subtract)
+    ts(B("LT0"), B("XL"), 1, A_.bitwise_and)
+    ts(B("LT1"), B("LT0"), -2.0, A_.mult, 1.0, A_.add)
+    for b in BAT:
+        a0, n = BAT[b]
+        q0, nq = a0 // 16, n // 16
+        vcopy(B("i%s0" % b, 2 * n, 2 * n + nq), B("XL", q0, q0 + nq))
+        tt(B("i%s0" % b, 2 * n + nq, 2 * n + 2 * nq), B("XL", q0, q0 + nq), B("LT1", q0, q0 + nq), A_.add)
+
+    def late_constants():
+        ts(B("BOV"), B("BO"), -1024.0, A_.mult)
+        ts(B("BOS"), B("BO"), -16.0, A_.mult)
+        vcopy(B("BOH"), B("BO"))
+        vcopy(B("IDH"), B("IDN"))
+        ts(B("OHT"), B("JT"), B("PC", 0, 1), A_.is_equal)
+        ts(B("CW"), B("CW0"), B("PC", 3, 4), A_.add)
+        for q, c0, w in ((0, 0, 32), (1, 32, 32), (2, 64, 64), (3, 128, 64)):
+            ts(B("LMT", c0, c0 + w), B("B64", 0, w), B("PC", 4 + q, 5 + q), A_.is_lt, B("PC", 8 + q, 9 + q), A_.mult)
+
+    def step1(t, b):
+        a0, n = BAT[b]
+        nq = n // 16
+        I, O = "i%s%d" % (b, t), "o%s%d" % (b, t)
+        return [
+            lambda: vcopy(B("LL" + b), B(I, 2 * n, 2 * n + 2 * nq)),
+            lambda: vgat(B("XV" + b), B("VAL", 0, 2048), B("LL" + b)),
+            lambda: tt(B("LE" + b), B("XV" + b, 0, n), B("XV" + b, n, 2 * n), A_.is_lt),
+            lambda: mm(B("psR", 0, n), B("BO"), B("LE" + b), True, True),
+            lambda: tt(B("DMC" + b), B(I, n, 2 * n), B(I, 0, n), A_.subtract),
+            lambda: ts(B("FL" + b), B("psR", 0, n), 8.5, A_.is_ge),
+            lambda: tt(B("T2" + b), B("FL" + b), B("DMC" + b), A_.mult),
+            lambda: tt(B(O, n, 2 * n), B("T2" + b), B(I, 0, n), A_.add),
+            lambda: vcopy(B("CU" + b), B(O, n, 2 * n)),
+        ]
+
+    def image(b, x0, x1):
+        a0 = BAT[b][0]
+        vgat(B("IMG", 16 * x0, 16 * x1), B("PT"), B("CU" + b, x0 - a0, x1 - a0))
+
+    def imf(x0, x1):
+        vcopy(B("IMF", 16 * x0, 16 * x1), B("IMG", 16 * x0, 16 * x1))
+
+    def values(f, x0, x1):
+        f(B("W", 256 * x0, 256 * x1), B("VAL", 0, 2048), B("IMG", 16 * x0, 16 * x1))
+
+    def scans(c):
+        p = c & 1
+        sb, yb = T["SB%d" % p], T["YB%d" % p]
+        wr = ("W", 4096 * c, 4096 * (c + 1))
+
+        def one(j):
+            op("v", lambda: V.tensor_tensor_scan(sb[:, 1:257, j], T.W[:, 4096 * c + j:4096 * (c + 1):16], T.MSK[:], 0.0, A_.max, A_.mult),
+               [wr, ("MSK", 0, 256)], [("SB%d.%d" % (p, j), 1, 257)])
+
+        def two(j):
+            op("v", lambda: V.tensor_tensor_scan(yb[:, :, j], T.W[:, 4096 * c + j:4096 * (c + 1):16], sb[:, 0:256, j], 0.0, A_.max, A_.min),
+               [wr, ("SB%d.%d" % (p, j), 0, 256)], [("YB%d.%d" % (p, j), 0, 256)])
+        out = [lambda: one(0)]
+        for j in range(1, 16):
+            out.append(lambda j=j: one(j))
+            out.append(lambda j=j: two(j - 1))
+        out.append(lambda: two(15))
+        return out
+
+    def diff(c):
+        p = c & 1
+        o = B("psD%d" % p, 0, 256)
+        op("t", lambda: TE.matmul(o[0], T.IDN[:], T["SB%d" % p][:, 16:257:16, :], True, False),
+           [("IDN", 0, 128)] + [("SB%d.%d" % (p, j), 16, 257) for j in range(16)], [o[1]])
+        op("t", lambda: TE.matmul(o[0], T.IDN[:], T["YB%d" % p][:, 15:256:16, :], False, True),
+           [("IDN", 0, 128)] + [("YB%d.%d" % (p, j), 15, 256) for j in range(16)], [o[1]])
+
+    def unit(t, c, q):
+        i, o = B("psD%d" % (c & 1), 0, 256), B("U", 256 * c, 256 * c + 256)
+        if q == "v":
+            ts(o, i, -float(MT[t]), A_.is_lt)
+        else:
+            act(o, i, -1000.0, -1000.0 * (MT[t] + 0.5), F.Sigmoid)
+
+    def votes(c):
+        o, c0 = B("psV%d" % (c & 1), 0, 256), 256 * (c % 2)
+        mm(o, B("E0"), B("A16", c0, c0 + 256), True, False)
+        mm(o, B("E0"), B("JT", 0, 256), False, False)
+        mm(o, B("BOV"), B("U", 256 * c, 256 * c + 256), False, True)
+
+    def scanmin(o, i):
+        n = o[1][2] - o[1][1]
+        m = B("MKK", 0, n)
+        op("v", lambda: V.tensor_tensor_scan(o[0], m[0], i[0], 0.0, A_.mult, A_.min), [m[1], i[1]], [o[1]])
+
+    def best(c):
+        scanmin(B("K1", 256 * c, 256 * c + 256), B("psV%d" % (c & 1), 0, 256))
+
+    def post(t, b):
+        a0, n = BAT[b]
+        nq, e0, e1, w, m0 = n // 16, 16 * a0, 16 * (a0 + n), a0 + n, 2 * a0
+        I, O = "i%s%d" % (b, t), "o%s%d" % (b, t)
+        km = lambda: B("K1", e0 + 15, e1, 16)
+        L = []
+        ad = L.append
+        ad(lambda: vcopy(B("KI" + b), km()))
+        ad(lambda: ts(B("QI" + b), B("KI" + b), 1023, A_.bitwise_and))
+        ad(lambda: vcopy(B("LU" + b), B("QI" + b)))
+        ad(lambda: sgat(B("UX", e0, e1), B("U", e0, e1), B("LU" + b)))
+        ad(lambda: tt(B("WI" + b), B("QI" + b), B("CW", 0, n), A_.add))
+        ad(lambda: ts(B("PRO", a0, a0 + n), km(), B("THR", 0, 1), A_.is_lt))
+        ad(lambda: vcopy(B("LW" + b), B("WI" + b)))
+        ad(lambda: ttg(B("MK", e0, e1), B("OHT"), B("LU" + b), B("IMF", e0, e1), A_.mult))
+
+        def newc():
+            for k in range(16):
+                mm(B("psN", 0, n), B("SEL", 128 * k, 128 * k + 128), B("MK", e0 + k, e1, 16), k == 0, k == 15)
+        ad(newc)
+        ad(lambda: ttg(B("PR", e0, e1), B("W", 16 * e0, 16 * e1), B("LW" + b), B("UX", e0, e1), A_.mult))
+
+        def sums():
+            mm(B("psS"), B("E0"), B("JT"), True, False)
+            mm(B("psS"), B("BOS"), B("PR", e0, e1), False, True)
+        ad(sums)
+        ad(lambda: ts(B("NP" + b), B("PRO", a0, a0 + n), -1.0, A_.mult, 1.0, A_.add))
+        ad(lambda: tt(B("NCG" + b), B("psN", 0, n), B("PRO", a0, a0 + n), A_.mult))
+        ad(lambda: tt(B("PEN" + b), B("NP" + b), B("PENC", a0, a0 + n), A_.mult))
+        ad(lambda: tt(B("DN" + b), B(I, n, 2 * n), B("NP" + b), A_.mult))
+        ad(lambda: scanmin(B("K2", e0, e1), B("psS")))
+        ad(lambda: vcopy(B("K2I" + b), B("K2", e0 + 15, e1, 16)))
+        ad(lambda: ts(B("KR" + b), B("K2I" + b), 15, A_.bitwise_and))
+        ad(lambda: ts(B("OHK" + b), B("KR" + b), B("PC", 0, 1), A_.is_equal))
+        ad(lambda: tt(B("XX" + b), B("OHK" + b), B("NCG" + b), A_.mult))
+
+        def marks():
+            mm(B("psR", 0, n), B("IDH"), B("PEN" + b), True, False)
+            mm(B("psR", 0, n), B("BOH"), B("XX" + b), False, True)
+        ad(marks)
+        ad(lambda: tt(B(O, 0, n), B("NCG" + b), B("DN" + b), A_.add))
+        ad(lambda: tt(B("DM" + b), B("psR", 0, n), B("OHT", 0, n), A_.mult))
+        ad(lambda: ts(B("PREP", a0, a0 + n), B("psR", 0, n), 0.49994, A_.mult, MAGIC, A_.add))
+        for q in range(nq):
+            ad(lambda q=q: red(B("NL" + b, q, q + 1), B("DM" + b, 16 * q, 16 * q + 16), A_.add))
+        ad(lambda: ts(B("PCL" + b), B("NL" + b, 0, nq), 0.49994, A_.mult, MAGIC, A_.add))
+        for q in range(nq):
+            ad(lambda q=q: ts(B("EQ" + b, w * q, w * q + w), B("PREP", 0, w), B("PCL" + b, q, q + 1), A_.is_equal))
+        ad(lambda: ts(B("FP" + b), B("PCL" + b), MAGIC, A_.subtract, 4.0, A_.mult))
+        ad(lambda: tt(B("EM" + b, 0, nq * w), B("EQ" + b, 0, nq * w), B("LMT", m0, m0 + nq * w), A_.mult))
+        ad(lambda: tt(B("LP" + b), B("FP" + b), B("NL" + b, 0, nq), A_.subtract))
+        ad(lambda: ts(B("NL" + b, nq, 2 * nq), B("LP" + b), 1.0, A_.add))
+        for q in range(nq):
+            ad(lambda q=q: red(B("DV" + b, q, q + 1), B("EM" + b, w * q, w * q + w), A_.max))
+        ad(lambda: ts(B("DV" + b, nq, 2 * nq), B("DV" + b, 0, nq), 1.0 + 2.0 ** -11, A_.mult))
+        ad(lambda: tt(B("OL" + b), B("NL" + b), B("DV" + b), A_.max))
+        ad(lambda: vcopy(B("EL" + b), B("OL" + b)))
+        ad(lambda: ttg(B("YE" + b), B("VAL"), B("EL" + b), B("DC"), A_.add))
+        ad(lambda: ts(B("ZE" + b), B("YE" + b), 255.0, A_.min, 0.0, A_.max))
+
+        def put():
+            x, e, z = B("VAL"), B("EL" + b), B("ZE" + b)
+            op("v", lambda: V.tensor_copy(x[0].indirect(e[0]), z[0]), [e[1], z[1]], [x[1]])
+        ad(put)
+        return L
+
+    def newmarks(t, b):
+        n = BAT[b][1]
+        I, O = "i%s%d" % (b, t), "o%s%d" % (b, t)
+        old = lambda: B(I, 2 * n, 2 * n + n // 8)
+        return [
+            lambda: ts(B("KP" + b), B("NL" + b), 2047.5, A_.is_lt),
+            lambda: tt(B("DL" + b), B("NL" + b), old(), A_.subtract),
+            lambda: tt(B("DK" + b), B("DL" + b), B("KP" + b), A_.mult),
+            lambda: tt(B(O, 2 * n, 2 * n + n // 8), B("DK" + b), old(), A_.add),
+        ]
+
+    def parity(t):
+        return [
+            lambda: red(B("THR", 1, 2), B("PRO"), A_.add),
+            lambda: vcopy(B("TI", 0, 1), B("THR", 1, 2)),
+            lambda: ts(B("TI", 1, 2), B("TI", 0, 1), 1, A_.bitwise_and),
+            lambda: ts(B("THR", 0, 1), B("TI", 1, 2), -1024.0, A_.mult, -1024.0 * (AT[t] - 1), A_.add),
+        ]
+
+    src, hand, dst = _route(rank, T, topo)
+    sent = [0]
+
+    def send(t, b):
+        if t == NR_ - 1:
+            return
+        o = B("o%s%d" % (b, t))
+        need("g", [o[1]], [])
+        to = hand if hand is not None else dst
+        sent[0] += _send(g, T, topo, core, to, o[0], "i%s%d" % (b, t + 1), "a%s%d" % (b, t + 1))
+
+    into = _route((rank - 3) % len(T.cores), T, topo)
+    arr = _mask(into[1] if into[1] is not None else into[0], core, topo)[1]
+
+    def arrive(t):
+        for b in BAT:
+            i, sem = B("i%s%d" % (b, t)), "a%s%d" % (b, t)
+            total[sem] = arr
+            note("rem" + sem, [], [i[1]], (sem, arr))
+
+    def mix(a, c, x0=0.0):
+        k = 0
+        for i, f in enumerate(a):
+            f()
+            want = int(max(((i + 1) / len(a) - x0) / (1.0 - x0), 0.0) * len(c) + 1e-6)
+            while k < want:
+                c[k]()
+                k += 1
+        while k < len(c):
+            c[k]()
+            k += 1
+
+    rest = []
+    for t in range(NR_):
+        if t:
+            arrive(t)
+        for f in step1(t, "A"):
+            f()
+        image("A", 0, 16)
+        values(sgat, 0, 16 - NV)
+        for f in rest:
+            f()
+        if t == 0:
+            late_constants()
+        values(vgat, 16 - NV, 16)
+        image("A", 16, 32)
+        values(sgat, 16, 32)
+        imf(0, 32)
+        mix(scans(0), (parity(t) if t else []) + step1(t, "B"), 0.5)
+        image("B", 32, 48)
+        values(sgat, 32, 40)
+        diff(0)
+        unit(t, 0, "s")
+        votes(0)
+        values(sgat, 40, 48)
+        image("B", 48, 64)
+        imf(32, 64)
+        mix(scans(1), [lambda: best(0)], 0.3)
+        diff(1)
+        unit(t, 1, "v")
+        votes(1)
+        if t == 0:
+            vcopy(B("SEL"), B("SL0"))
+        best(1)
+        chain = post(t, "A") + newmarks(t, "A") + [lambda: send(t, "A")]
+        cut = len(post(t, "A")) - 3
+        for f in chain[:4]:
+            f()
+        values(sgat, 48, 64)
+        for f in chain[4:PRE]:
+            f()
+        mix(scans(2), chain[PRE:cut] + chain[cut + 3:])
+        diff(2)
+        unit(t, 2, "s")
+        votes(2)
+        mix(scans(3), [lambda: best(2)] + chain[cut:cut + 3], 0.1)
+        diff(3)
+        unit(t, 3, "v")
+        votes(3)
+        best(3)
+        for f in post(t, "B"):
+            f()
+        rest = newmarks(t, "B") + [lambda t=t: send(t, "B")]
+    for f in rest:
+        f()
+
+    t = NR_ - 1
+    v, c, d, l = B("VAL", 0, 2048), B("YC"), B("YD"), B("YL")
+    dma("y", T.yv[:], v[0], [v[1]], [], "st0")
+    flip("Z", "ZT", lane16("o", t, 0), lambda q: B("YC", q, 64, 4))
+    dma("y", T.yc[:], c[0], [c[1]], [], "st1")
+    flip("Z2", "ZT2", lane16("o", t, 1), lambda q: B("YD", q, 64, 4))
+    dma("s", T.yd[:], d[0], [d[1]], [], "st2")
+    for b in BAT:
+        a0, n = BAT[b]
+        vcopy(B("YL", a0 // 16, (a0 + n) // 16), B("o%s%d" % (b, t), 2 * n, 2 * n + n // 16))
+    dma("y", T.yl[:], l[0], [l[1]], [], "st3")
+    total["ls"] = sent[0]
+    for s in total:
+        if total[s]:
+            g.wait_ge(T.sem[s], total[s])

@@ -12,11 +12,11 @@ MAGIC = 12582912.0
 _SIZE = {"float32": 4, "int32": 4, "uint16": 2, "float16": 2, "bfloat16": 2}
 SCRATCH = {}
 for _d, _names in (("int32", "GEN 1024 CW0 64 CW 64 PI 8 XC 64 XD 64 XL 4 LT0 4 LT1 4 TI 2"),
-                   ("float32", "GM 1024 PM 1024 PT 2048 K1 1024 K2 1024 B64 64 PENC 64 LMT 192 PC 16 DC 64 Z 128 ZT 128 Z2 128 ZT2 128 "
-                               "YC 64 YD 64 YL 4 PREP 64 PRO 64 THR 4"),
+                   ("float32", "GM 1024 PM 1024 PT 2048 IFB 512 K1 1024 K2 1024 B64 64 PENC 64 LMT 192 PC 16 DC 64 Z 128 ZT 128 "
+                               "Z2 128 ZT2 128 FX 64 FX2 64 YC 64 YD 64 YL 4 PREP 64 THR 4"),
                    ("bfloat16", "VAL 2176 W 16384 U 1024 UX 1024 PR 1024 MSK 256 MKK 512 ONE 128 BO 128 B1 128 BOV 128 BOS 128 IDN 128 "
-                                "E0 128 SL0 2048 JT 512 A16 512 OHT 512"),
-                   ("float16", "IMF 1024 MK 1024 BOH 128 IDH 128 SEL 2048"), ("uint16", "IMG 1024")):
+                                "E0 128 SL0 2048 JT 512 A16 512 OHT 512 PRO 64 NP 64"),
+                   ("float16", "IFA 512 MK 1024 BOH 128 IDH 128 SEL 2048"), ("uint16", "IMG 1024")):
     _w = _names.split()
     for _i in range(0, len(_w), 2):
         SCRATCH[_w[_i]] = ("sbuf", [128, int(_w[_i + 1])], _d)
@@ -42,8 +42,8 @@ def _declare():
                          ("bfloat16", (("XV", 2 * n), ("LE", n), ("ZE", 2 * n))),
                          ("int32", (("KI", n), ("QI", n), ("WI", n), ("K2I", n), ("KR", n))),
                          ("float16", (("PEN", n), ("NCG", n), ("XX", n))),
-                         ("float32", (("DMC", n), ("FL", n), ("T2", n), ("NP", n), ("DN", n), ("OHK", n), ("DM", n), ("NL", 2 * nq),
-                                      ("PCL", nq), ("EQ", 64 * nq), ("EM", 64 * nq), ("DV", 2 * nq), ("FP", nq), ("LP", nq),
+                         ("float32", (("DMC", n), ("FL", n), ("T2", n), ("NM", nq), ("DN", n), ("OHK", n), ("DM", n), ("NL", 2 * nq),
+                                      ("PCL", nq), ("EQ", 64 * nq), ("EM", 64 * nq), ("DV", 2 * nq), ("FP", nq),
                                       ("OL", 2 * nq), ("YE", 2 * n), ("KP", 2 * nq), ("DL", 2 * nq), ("DK", 2 * nq)))):
             for nm, w in names:
                 al = 64 // _SIZE[d]
@@ -89,6 +89,21 @@ def _relay(g, core, T, topo):
                 g.wait_ge(T.sem[sem], _mask(s, h, topo)[1])
                 tot += _send(g, T, topo, core, d, T[nm][:], nm, sem)
         g.wait_ge(T.sem["ls"], tot)
+
+
+def _weave(a, c, x0=0.0):
+    L, k = [], 0
+    for i, f in enumerate(a):
+        L.append(f)
+        want = int(max(((i + 1) / len(a) - x0) / (1.0 - x0), 0.0) * len(c) + 1e-6)
+        L += c[k:want]
+        k = max(k, want)
+    return L + c[k:]
+
+
+def _go(L):
+    for f in L:
+        f()
 
 
 def rank_program(g, core, T, topo):
@@ -173,6 +188,12 @@ def rank_program(g, core, T, topo):
         else:
             op("v", lambda: V.tensor_scalar(o[0], a[0], x1, x2, f1, f2), rd, [o[1]])
 
+    def lin(b, o, i, scale, bias):
+        if b == "B":
+            act(o, i, scale, bias)
+        else:
+            ts(o, i, scale, A_.mult, bias, A_.add)
+
     def red(o, a, f):
         op("v", lambda: V.tensor_reduce(o[0], a[0], X_, f), [a[1]], [o[1]])
 
@@ -198,27 +219,6 @@ def rank_program(g, core, T, topo):
 
     iota(B("PI", 0, 1), [[1, 1]], 0, 1, True)
     ms(B("ONE"), 1.0)
-    ms(B("SL0"), 1.0)
-    for p in (0, 1):
-        op("v", lambda p=p: V.memset(T["SB%d" % p][:, 0, :], 0.0), [], [("SB%d.%d" % (p, j), 0, 1) for j in range(16)])
-    ms(B("MSK"), 1.0)
-    ms(B("MKK"), 1.0)
-    ms(B("VAL", 2048, 2176), 0.0)
-    ms(B("MSK", 15, 256, 16), -1.0)
-    ms(B("MKK", 0, 512, 16), 0.0)
-    ms(B("DC", 0, 32), 32.0)
-    ms(B("DC", 32, 64), -32.0)
-    ts(B("PI", 1, 2), B("PI", 0, 1), 15, A_.bitwise_and)
-    ts(B("PI", 2, 3), B("PI", 0, 1), 16, A_.bitwise_and)
-    vcopy(B("PC", 0, 1), B("PI", 1, 2))
-    ts(B("PC", 1, 2), B("PI", 2, 3), 0.0, A_.is_equal)
-    ts(B("PC", 2, 3), B("PI", 2, 3), 16.0, A_.is_equal)
-    ts(B("PC", 3, 4), B("PC", 0, 1), 16.0, A_.mult)
-    for q in range(4):
-        ts(B("PC", 4 + q, 5 + q), B("PC", 0, 1), 16.0 * q, A_.add)
-    for q in range(4):
-        ts(B("PC", 8 + q, 9 + q), B("PC", 4 + q, 5 + q), 2.0, A_.mult, 2048.0, A_.add)
-    ms(B("THR", 0, 1), -1024.0 * (AT[0] - 1))
     asel(B("B1"), B("ONE"), [[-16, 8], [0, 16]], A_.is_ge, 0, 1)
     asel(B("BO"), B("B1"), [[16, 8], [0, 16]], A_.is_ge, 15, -1)
     asel(B("IDN"), B("ONE"), [[-1, 128]], A_.is_equal, 0, 1)
@@ -228,18 +228,41 @@ def rank_program(g, core, T, topo):
     iota(B("CW0"), [[240, 64]], 0, 0, True)
     iota(B("B64"), [[1, 64]], 0, 0)
     iota(B("PENC"), [[2, 64]], 2048, 0)
-    asel(B("SL0"), B("SL0"), [[1, 16], [0, 8], [-1, 16]], A_.is_equal, 0, 0)
-    asel(B("SL0"), B("SL0"), [[0, 16], [-16, 8], [0, 16]], A_.is_ge, 0, 1)
-    asel(B("SL0"), B("SL0"), [[0, 16], [16, 8], [0, 16]], A_.is_ge, 15, -1)
+    ms(B("VAL", 2048, 2176), 0.0)
+    ts(B("PI", 1, 2), B("PI", 0, 1), 15, A_.bitwise_and)
+    ts(B("PI", 2, 3), B("PI", 0, 1), 16, A_.bitwise_and)
+    ms(B("DC", 0, 32), 32.0)
+    vcopy(B("PC", 0, 1), B("PI", 1, 2))
+    ts(B("PC", 1, 2), B("PI", 2, 3), 0.0, A_.is_equal)
+    ts(B("PC", 2, 3), B("PI", 2, 3), 16.0, A_.is_equal)
+    ts(B("PC", 3, 4), B("PC", 0, 1), 16.0, A_.mult)
+    for q in range(4):
+        ts(B("PC", 4 + q, 5 + q), B("PC", 0, 1), 16.0 * q, A_.add)
+    for q in range(4):
+        ts(B("PC", 8 + q, 9 + q), B("PC", 4 + q, 5 + q), 2.0, A_.mult, 2048.0, A_.add)
+    for p in (0, 1):
+        op("v", lambda p=p: V.memset(T["SB%d" % p][:, 0, :], 0.0), [], [("SB%d.%d" % (p, j), 0, 1) for j in range(16)])
+    ms(B("DC", 32, 64), -32.0)
+    ms(B("THR", 2, 3), -1024000.0 * (AT[0] - 1) - 500.0)
+    ms(B("THR", 3, 4), 1024000.0 * (AT[0] - 1) + 500.0)
+    ms(B("MSK"), 1.0)
+    ms(B("MKK"), 1.0)
 
-    def flip(Z, ZT, src, dst):
-        for q in range(4):
-            for h in range(2):
-                ts(B(Z, 32 * q + 16 * h, 32 * q + 16 * h + 16), src(q), B("PC", 1 + h, 2 + h), A_.mult)
-        a, b = B(Z), B(ZT)
-        op("v", lambda: V.transpose(b[0], a[0]), [a[1]], [b[1]])
-        for q in range(4):
-            tt(dst(q), B(ZT, 32 * q, 32 * q + 16), B(ZT, 32 * q + 16, 32 * q + 32), A_.add)
+    def flip(q_, Z, ZT, src, dst):
+        def blocks():
+            for q in range(4):
+                for h in range(2):
+                    o, i, m = B(Z, 32 * q + 16 * h, 32 * q + 16 * h + 16), src(q), B("PC", 1 + h, 2 + h)
+                    if q_ == "s":
+                        op("s", lambda: S.activation(o[0], i[0], F.Copy, scale=m[0]), [i[1], m[1]], [o[1]])
+                    else:
+                        ts(o, i, m, A_.mult)
+
+        def turn():
+            a, b = B(Z), B(ZT)
+            op("v", lambda: V.transpose(b[0], a[0]), [a[1]], [b[1]])
+        return [blocks, turn] + [lambda q=q: tt(dst(q), B(ZT, 32 * q, 32 * q + 16), B(ZT, 32 * q + 16, 32 * q + 32), A_.add)
+                                 for q in range(4)]
 
     def lane16(pre, t, part):
         def f(q):
@@ -248,27 +271,41 @@ def rank_program(g, core, T, topo):
             return B("%s%s%d" % (pre, b, t), c, c + 16)
         return f
 
-    flip("Z", "ZT", lambda q: B("XC", q, 64, 4), lane16("i", 0, 0))
+    vcopy(B("FX"), B("XC"))
+    fc = flip("s", "Z", "ZT", lambda q: B("FX", q, 64, 4), lane16("i", 0, 0))
+    fd = flip("v", "Z2", "ZT2", lambda q: B("FX2", q, 64, 4), lane16("i", 0, 1))
+    fc[0]()
+    vcopy(B("FX2"), B("XD"))
     HF = ((0, 512), (512, 1024))
     for c0, c1 in HF:
         vcopy(B("PT", 2 * c0, 2 * c1, 2), B("GEN", c0, c1))
     for i, (c0, c1) in enumerate(HF):
         act(B("PM", c0, c1), B("PT", 2 * c0, 2 * c1, 2), 0.49994, MAGIC)
         act(B("psD%d" % i), B("PM", c0, c1), 4.0, -4.0 * MAGIC)
-    for c0, c1 in HF:
-        ts(B("GM", c0, c1), B("GEN", c0, c1), 1.0, A_.subtract)
-    flip("Z2", "ZT2", lambda q: B("XD", q, 64, 4), lane16("i", 0, 1))
-    for i, (c0, c1) in enumerate(HF):
-        tt(B("PT", 2 * c0 + 1, 2 * c1, 2), B("psD%d" % i), B("GM", c0, c1), A_.subtract)
+    _go(fc[1:2])
+    ts(B("GM", 0, 512), B("GEN", 0, 512), 1.0, A_.subtract)
+    _go(fc[2:])
+    ts(B("GM", 512, 1024), B("GEN", 512, 1024), 1.0, A_.subtract)
+    _go(fd)
     ts(B("LT0"), B("XL"), 1, A_.bitwise_and)
+    for b in BAT:
+        a0, n = BAT[b]
+        vcopy(B("i%s0" % b, 2 * n, 2 * n + n // 16), B("XL", a0 // 16, (a0 + n) // 16))
     ts(B("LT1"), B("LT0"), -2.0, A_.mult, 1.0, A_.add)
+    tt(B("PT", 1, 1024, 2), B("psD0"), B("GM", 0, 512), A_.subtract)
     for b in BAT:
         a0, n = BAT[b]
         q0, nq = a0 // 16, n // 16
-        vcopy(B("i%s0" % b, 2 * n, 2 * n + nq), B("XL", q0, q0 + nq))
         tt(B("i%s0" % b, 2 * n + nq, 2 * n + 2 * nq), B("XL", q0, q0 + nq), B("LT1", q0, q0 + nq), A_.add)
+    tt(B("PT", 1025, 2048, 2), B("psD1"), B("GM", 512, 1024), A_.subtract)
 
     def late_constants():
+        ms(B("SL0"), 1.0)
+        asel(B("SL0"), B("SL0"), [[1, 16], [0, 8], [-1, 16]], A_.is_equal, 0, 0)
+        asel(B("SL0"), B("SL0"), [[0, 16], [-16, 8], [0, 16]], A_.is_ge, 0, 1)
+        asel(B("SL0"), B("SL0"), [[0, 16], [16, 8], [0, 16]], A_.is_ge, 15, -1)
+        ms(B("MSK", 15, 256, 16), -1.0)
+        ms(B("MKK", 0, 512, 16), 0.0)
         ts(B("BOV"), B("BO"), -1024.0, A_.mult)
         ts(B("BOS"), B("BO"), -16.0, A_.mult)
         vcopy(B("BOH"), B("BO"))
@@ -298,8 +335,12 @@ def rank_program(g, core, T, topo):
         a0 = BAT[b][0]
         vgat(B("IMG", 16 * x0, 16 * x1), B("PT"), B("CU" + b, x0 - a0, x1 - a0))
 
-    def imf(x0, x1):
-        vcopy(B("IMF", 16 * x0, 16 * x1), B("IMG", 16 * x0, 16 * x1))
+    def imf(b):
+        a0, n = BAT[b]
+        if b == "A":
+            vcopy(B("IFA"), B("IMG", 16 * a0, 16 * (a0 + n)))
+        else:
+            sgat(B("IFB"), B("PT"), B("CU" + b))
 
     def values(f, x0, x1):
         f(B("W", 256 * x0, 256 * x1), B("VAL", 0, 2048), B("IMG", 16 * x0, 16 * x1))
@@ -352,71 +393,82 @@ def rank_program(g, core, T, topo):
     def best(c):
         scanmin(B("K1", 256 * c, 256 * c + 256), B("psV%d" % (c & 1), 0, 256))
 
-    def post(t, b):
+    def post(t, b, x0, x1):
         a0, n = BAT[b]
         nq, e0, e1, w, m0 = n // 16, 16 * a0, 16 * (a0 + n), a0 + n, 2 * a0
         I, O = "i%s%d" % (b, t), "o%s%d" % (b, t)
         km = lambda: B("K1", e0 + 15, e1, 16)
-        L = []
-        ad = L.append
-        ad(lambda: vcopy(B("KI" + b), km()))
-        ad(lambda: ts(B("QI" + b), B("KI" + b), 1023, A_.bitwise_and))
-        ad(lambda: vcopy(B("LU" + b), B("QI" + b)))
-        ad(lambda: sgat(B("UX", e0, e1), B("U", e0, e1), B("LU" + b)))
-        ad(lambda: tt(B("WI" + b), B("QI" + b), B("CW", 0, n), A_.add))
-        ad(lambda: ts(B("PRO", a0, a0 + n), km(), B("THR", 0, 1), A_.is_lt))
-        ad(lambda: vcopy(B("LW" + b), B("WI" + b)))
-        ad(lambda: ttg(B("MK", e0, e1), B("OHT"), B("LU" + b), B("IMF", e0, e1), A_.mult))
+
+        def promoted():
+            for o, f, c in (("PRO", -1000.0, 2), ("NP", 1000.0, 3)):
+                x, y, z = B(o, a0, a0 + n), km(), B("THR", c, c + 1)
+                op("s", lambda: S.activation(x[0], y[0], F.Sigmoid, bias=z[0], scale=f), [y[1], z[1]], [x[1]])
 
         def newc():
             for k in range(16):
                 mm(B("psN", 0, n), B("SEL", 128 * k, 128 * k + 128), B("MK", e0 + k, e1, 16), k == 0, k == 15)
-        ad(newc)
-        ad(lambda: ttg(B("PR", e0, e1), B("W", 16 * e0, 16 * e1), B("LW" + b), B("UX", e0, e1), A_.mult))
 
         def sums():
             mm(B("psS"), B("E0"), B("JT"), True, False)
             mm(B("psS"), B("BOS"), B("PR", e0, e1), False, True)
-        ad(sums)
-        ad(lambda: ts(B("NP" + b), B("PRO", a0, a0 + n), -1.0, A_.mult, 1.0, A_.add))
-        ad(lambda: tt(B("NCG" + b), B("psN", 0, n), B("PRO", a0, a0 + n), A_.mult))
-        ad(lambda: tt(B("PEN" + b), B("NP" + b), B("PENC", a0, a0 + n), A_.mult))
-        ad(lambda: tt(B("DN" + b), B(I, n, 2 * n), B("NP" + b), A_.mult))
-        ad(lambda: scanmin(B("K2", e0, e1), B("psS")))
-        ad(lambda: vcopy(B("K2I" + b), B("K2", e0 + 15, e1, 16)))
-        ad(lambda: ts(B("KR" + b), B("K2I" + b), 15, A_.bitwise_and))
-        ad(lambda: ts(B("OHK" + b), B("KR" + b), B("PC", 0, 1), A_.is_equal))
-        ad(lambda: tt(B("XX" + b), B("OHK" + b), B("NCG" + b), A_.mult))
 
         def marks():
             mm(B("psR", 0, n), B("IDH"), B("PEN" + b), True, False)
             mm(B("psR", 0, n), B("BOH"), B("XX" + b), False, True)
-        ad(marks)
-        ad(lambda: tt(B(O, 0, n), B("NCG" + b), B("DN" + b), A_.add))
-        ad(lambda: tt(B("DM" + b), B("psR", 0, n), B("OHT", 0, n), A_.mult))
-        ad(lambda: ts(B("PREP", a0, a0 + n), B("psR", 0, n), 0.49994, A_.mult, MAGIC, A_.add))
-        for q in range(nq):
-            ad(lambda q=q: red(B("NL" + b, q, q + 1), B("DM" + b, 16 * q, 16 * q + 16), A_.add))
-        ad(lambda: ts(B("PCL" + b), B("NL" + b, 0, nq), 0.49994, A_.mult, MAGIC, A_.add))
-        for q in range(nq):
-            ad(lambda q=q: ts(B("EQ" + b, w * q, w * q + w), B("PREP", 0, w), B("PCL" + b, q, q + 1), A_.is_equal))
-        ad(lambda: ts(B("FP" + b), B("PCL" + b), MAGIC, A_.subtract, 4.0, A_.mult))
-        ad(lambda: tt(B("EM" + b, 0, nq * w), B("EQ" + b, 0, nq * w), B("LMT", m0, m0 + nq * w), A_.mult))
-        ad(lambda: tt(B("LP" + b), B("FP" + b), B("NL" + b, 0, nq), A_.subtract))
-        ad(lambda: ts(B("NL" + b, nq, 2 * nq), B("LP" + b), 1.0, A_.add))
-        for q in range(nq):
-            ad(lambda q=q: red(B("DV" + b, q, q + 1), B("EM" + b, w * q, w * q + w), A_.max))
-        ad(lambda: ts(B("DV" + b, nq, 2 * nq), B("DV" + b, 0, nq), 1.0 + 2.0 ** -11, A_.mult))
-        ad(lambda: tt(B("OL" + b), B("NL" + b), B("DV" + b), A_.max))
-        ad(lambda: vcopy(B("EL" + b), B("OL" + b)))
-        ad(lambda: ttg(B("YE" + b), B("VAL"), B("EL" + b), B("DC"), A_.add))
-        ad(lambda: ts(B("ZE" + b), B("YE" + b), 255.0, A_.min, 0.0, A_.max))
 
         def put():
             x, e, z = B("VAL"), B("EL" + b), B("ZE" + b)
             op("v", lambda: V.tensor_copy(x[0].indirect(e[0]), z[0]), [e[1], z[1]], [x[1]])
-        ad(put)
-        return L
+        L = [
+            lambda: vcopy(B("KI" + b), km()),
+            lambda: ts(B("QI" + b), B("KI" + b), 1023, A_.bitwise_and),
+            lambda: vcopy(B("LU" + b), B("QI" + b)),
+            lambda: sgat(B("UX", e0, e1), B("U", e0, e1), B("LU" + b)),
+            lambda: tt(B("WI" + b), B("QI" + b), B("CW", 0, n), A_.add),
+            promoted,
+            lambda: vcopy(B("LW" + b), B("WI" + b)),
+            lambda: ttg(B("MK", e0, e1), B("OHT"), B("LU" + b), B("IF" + b), A_.mult),
+            newc,
+            lambda: ttg(B("PR", e0, e1), B("W", 16 * e0, 16 * e1), B("LW" + b), B("UX", e0, e1), A_.mult),
+            sums,
+            lambda: tt(B("PEN" + b), B("NP", a0, a0 + n), B("PENC", a0, a0 + n), A_.mult),
+            lambda: tt(B("DN" + b), B(I, n, 2 * n), B("NP", a0, a0 + n), A_.mult),
+            lambda: tt(B("NCG" + b), B("psN", 0, n), B("PRO", a0, a0 + n), A_.mult),
+            lambda: tt(B(O, 0, n), B("NCG" + b), B("DN" + b), A_.add),
+        ]
+        M = [
+            lambda: scanmin(B("K2", e0, e1), B("psS")),
+            lambda: vcopy(B("K2I" + b), B("K2", e0 + 15, e1, 16)),
+            lambda: ts(B("KR" + b), B("K2I" + b), 15, A_.bitwise_and),
+            lambda: ts(B("OHK" + b), B("KR" + b), B("PC", 0, 1), A_.is_equal),
+            lambda: tt(B("XX" + b), B("OHK" + b), B("NCG" + b), A_.mult),
+            marks,
+            lambda: tt(B("DM" + b), B("psR", 0, n), B("OHT", 0, n), A_.mult),
+            lambda: lin(b, B("PREP", a0, a0 + n), B("psR", 0, n), 0.49994, MAGIC),
+        ]
+        M += [lambda q=q: red(B("NL" + b, q, q + 1), B("DM" + b, 16 * q, 16 * q + 16), A_.add) for q in range(nq)]
+        M += [
+            lambda: ts(B("PCL" + b), B("NL" + b, 0, nq), 0.49994, A_.mult, MAGIC, A_.add),
+            lambda: lin(b, B("NM" + b), B("NL" + b, 0, nq), -1.0, 1.0),
+        ]
+        M += [lambda q=q: ts(B("EQ" + b, w * q, w * q + w), B("PREP", 0, w), B("PCL" + b, q, q + 1), A_.is_equal) for q in range(nq)]
+        M += [lambda: lin(b, B("FP" + b), B("PCL" + b), 4.0, -4.0 * MAGIC)]
+        N = [
+            lambda: tt(B("EM" + b, 0, nq * w), B("EQ" + b, 0, nq * w), B("LMT", m0, m0 + nq * w), A_.mult),
+            lambda: tt(B("NL" + b, nq, 2 * nq), B("FP" + b), B("NM" + b), A_.add),
+        ]
+        N += [lambda q=q: red(B("DV" + b, q, q + 1), B("EM" + b, w * q, w * q + w), A_.max) for q in range(nq)]
+        N += [
+            lambda: ts(B("DV" + b, nq, 2 * nq), B("DV" + b, 0, nq), 1.0 + 2.0 ** -11, A_.mult),
+            lambda: tt(B("OL" + b), B("NL" + b), B("DV" + b), A_.max),
+            lambda: vcopy(B("EL" + b), B("OL" + b)),
+        ]
+        E = [
+            lambda: ttg(B("YE" + b), B("VAL"), B("EL" + b), B("DC"), A_.add),
+            lambda: ts(B("ZE" + b), B("YE" + b), 255.0, A_.min, 0.0, A_.max),
+            put,
+        ]
+        return L + _weave(M, x0) + N[:2] + _weave(N[2:], x1), E
 
     def newmarks(t, b):
         n = BAT[b][1]
@@ -434,7 +486,8 @@ def rank_program(g, core, T, topo):
             lambda: red(B("THR", 1, 2), B("PRO"), A_.add),
             lambda: vcopy(B("TI", 0, 1), B("THR", 1, 2)),
             lambda: ts(B("TI", 1, 2), B("TI", 0, 1), 1, A_.bitwise_and),
-            lambda: ts(B("THR", 0, 1), B("TI", 1, 2), -1024.0, A_.mult, -1024.0 * (AT[t] - 1), A_.add),
+            lambda: ts(B("THR", 2, 3), B("TI", 1, 2), -1024000.0, A_.mult, -1024000.0 * (AT[t] - 1) - 500.0, A_.add),
+            lambda: ts(B("THR", 3, 4), B("TI", 1, 2), 1024000.0, A_.mult, 1024000.0 * (AT[t] - 1) + 500.0, A_.add),
         ]
 
     src, hand, dst = _route(rank, T, topo)
@@ -457,83 +510,68 @@ def rank_program(g, core, T, topo):
             total[sem] = arr
             note("rem" + sem, [], [i[1]], (sem, arr))
 
-    def mix(a, c, x0=0.0):
-        k = 0
-        for i, f in enumerate(a):
-            f()
-            want = int(max(((i + 1) / len(a) - x0) / (1.0 - x0), 0.0) * len(c) + 1e-6)
-            while k < want:
-                c[k]()
-                k += 1
-        while k < len(c):
-            c[k]()
-            k += 1
+    def store(q, y, nm, sem, c1):
+        o = B(nm, 0, c1)
+        dma(q, y[:], o[0], [o[1]], [], sem)
 
-    rest = []
+    def outputs(q, part, fx, z, zt, y, yd, sem):
+        t = NR_ - 1
+        L = [lambda b=b: vcopy(B(fx, BAT[b][0], sum(BAT[b])), B("o%s%d" % (b, t), part * BAT[b][1], (part + 1) * BAT[b][1])) for b in BAT]
+        return L + flip("s", z, zt, lambda x: B(fx, 16 * x, 16 * x + 16), lambda x: B(y, x, 64, 4)) + [lambda: store(q, yd, y, sem, 64)]
+
     for t in range(NR_):
+        last = t == NR_ - 1
         if t:
             arrive(t)
-        for f in step1(t, "A"):
-            f()
+        _go(step1(t, "A"))
         image("A", 0, 16)
         values(sgat, 0, 16 - NV)
-        for f in rest:
-            f()
+        image("A", 16, 32)
         if t == 0:
             late_constants()
         values(vgat, 16 - NV, 16)
-        image("A", 16, 32)
         values(sgat, 16, 32)
-        imf(0, 32)
-        mix(scans(0), (parity(t) if t else []) + step1(t, "B"), 0.5)
-        image("B", 32, 48)
+        imf("A")
+        _go(_weave(scans(0), (parity(t) if t else []) + step1(t, "B") + [lambda: image("B", 32, 48)], 0.3))
         values(sgat, 32, 40)
         diff(0)
         unit(t, 0, "s")
         votes(0)
         values(sgat, 40, 48)
-        image("B", 48, 64)
-        imf(32, 64)
-        mix(scans(1), [lambda: best(0)], 0.3)
+        _go(_weave(scans(1), [lambda: image("B", 48, 64), lambda: best(0)], 0.1))
         diff(1)
         unit(t, 1, "v")
         votes(1)
         if t == 0:
             vcopy(B("SEL"), B("SL0"))
         best(1)
-        chain = post(t, "A") + newmarks(t, "A") + [lambda: send(t, "A")]
-        cut = len(post(t, "A")) - 3
-        for f in chain[:4]:
-            f()
+        chain, late = post(t, "A", [], newmarks(t, "A"))
+        _go(chain[:6])
         values(sgat, 48, 64)
-        for f in chain[4:PRE]:
-            f()
-        mix(scans(2), chain[PRE:cut] + chain[cut + 3:])
+        imf("B")
+        _go(chain[6:PRE])
+        _go(_weave(scans(2), chain[PRE:] + [lambda: send(t, "A")]))
         diff(2)
         unit(t, 2, "s")
         votes(2)
-        mix(scans(3), [lambda: best(2)] + chain[cut:cut + 3], 0.1)
+        _go(_weave(scans(3), [lambda: best(2)], 0.2))
         diff(3)
+        late[0]()
         unit(t, 3, "v")
         votes(3)
+        _go(late[1:])
         best(3)
-        for f in post(t, "B"):
-            f()
-        rest = newmarks(t, "B") + [lambda t=t: send(t, "B")]
-    for f in rest:
-        f()
+        x0 = outputs("s", 1, "FX2", "Z2", "ZT2", "YD", T.yd, "st2") + outputs("y", 0, "FX", "Z", "ZT", "YC", T.yc, "st1") if last else []
+        chain, late = post(t, "B", x0, newmarks(t, "B"))
+        _go(chain)
+        send(t, "B")
+        _go(late)
 
-    t = NR_ - 1
-    v, c, d, l = B("VAL", 0, 2048), B("YC"), B("YD"), B("YL")
-    dma("y", T.yv[:], v[0], [v[1]], [], "st0")
-    flip("Z", "ZT", lane16("o", t, 0), lambda q: B("YC", q, 64, 4))
-    dma("y", T.yc[:], c[0], [c[1]], [], "st1")
-    flip("Z2", "ZT2", lane16("o", t, 1), lambda q: B("YD", q, 64, 4))
-    dma("s", T.yd[:], d[0], [d[1]], [], "st2")
+    store("y", T.yv, "VAL", "st0", 2048)
     for b in BAT:
         a0, n = BAT[b]
-        vcopy(B("YL", a0 // 16, (a0 + n) // 16), B("o%s%d" % (b, t), 2 * n, 2 * n + n // 16))
-    dma("y", T.yl[:], l[0], [l[1]], [], "st3")
+        vcopy(B("YL", a0 // 16, (a0 + n) // 16), B("o%s%d" % (b, NR_ - 1), 2 * n, 2 * n + n // 16))
+    store("s", T.yl, "YL", "st3", 4)
     total["ls"] = sent[0]
     for s in total:
         if total[s]:

from concourse.mybir import dt, AluOpType, AxisListType, ActivationFunctionType

A_ = AluOpType
F = ActivationFunctionType
X_ = AxisListType.X
NR_ = 5
BAT = {"A": (0, 32), "B": (32, 32)}
NV = 8
PRE = 8
MAGIC = 12582912.0

_SIZE = {"float32": 4, "int32": 4, "uint16": 2, "float16": 2, "bfloat16": 2}
SCRATCH = {}
for _d, _names in (("int32", "GEN 1024 CW0 64 CW 64 PI 8 XC 64 XD 64 XL 4 LT0 4 LT1 4 TI 2"),
                   ("float32", "GM 1024 PM 1024 PT 2048 IFB 512 K1 1024 K2 1024 B64 64 PENC 64 LMT 192 PC 16 DC 64 Z 128 ZT 128 "
                               "Z2 128 ZT2 128 FX 64 FX2 64 YC 64 YD 64 YL 4 PREP 64 THR 4"),
                   ("bfloat16", "VAL 2176 W 16384 U 1024 UX 1024 PR 1024 MSK 256 MKK 512 ONE 128 BO 128 B1 128 BOV 128 BOS 128 IDN 128 "
                                "E0 128 SL0 2048 JT 512 A16 512 OHT 512 PRO 64 NP 64"),
                   ("float16", "IFA 512 MK 1024 BOH 128 IDH 128 SEL 2048"), ("uint16", "IMG 1024")):
    _w = _names.split()
    for _i in range(0, len(_w), 2):
        SCRATCH[_w[_i]] = ("sbuf", [128, int(_w[_i + 1])], _d)
for _i in (0, 1):
    SCRATCH["SB%d" % _i] = ("sbuf", [128, 257, 16], "bfloat16")
    SCRATCH["YB%d" % _i] = ("sbuf", [128, 256, 16], "bfloat16")
for _n in "psD0 psD1 psV0 psV1 psS psN psR".split():
    SCRATCH[_n] = ("psum", [128, 512], "float32")
SEMAPHORES = "vc sc tc gc ls ld0 ld1 ld2 ld3 ld4 st0 st1 st2 st3".split()
_POS = {}


def _declare():
    tot = {}
    for b, (a0, n) in BAT.items():
        nq = n // 16
        for t in range(NR_):
            SCRATCH["i%s%d" % (b, t)] = ("sbuf", [128, 2 * n + 2 * nq], "float16")
            SCRATCH["o%s%d" % (b, t)] = ("sbuf", [128, 2 * n + 2 * nq], "float16")
            if t:
                SEMAPHORES.append("a%s%d" % (b, t))
        for d, names in (("uint16", (("LL", 2 * nq), ("CU", n), ("LU", n), ("LW", n), ("EL", 2 * nq))),
                         ("bfloat16", (("XV", 2 * n), ("LE", n), ("ZE", 2 * n))),
                         ("int32", (("KI", n), ("QI", n), ("WI", n), ("K2I", n), ("KR", n))),
                         ("float16", (("PEN", n), ("NCG", n), ("XX", n))),
                         ("float32", (("DMC", n), ("FL", n), ("T2", n), ("NM", nq), ("DN", n), ("OHK", n), ("DM", n), ("NL", 2 * nq),
                                      ("PCL", nq), ("EQ", 64 * nq), ("EM", 64 * nq), ("DV", 2 * nq), ("FP", nq),
                                      ("OL", 2 * nq), ("YE", 2 * n), ("KP", 2 * nq), ("DL", 2 * nq), ("DK", 2 * nq)))):
            for nm, w in names:
                al = 64 // _SIZE[d]
                _POS[nm + b] = ("pk_" + d, tot.get(d, 0), w)
                tot[d] = tot.get(d, 0) + (w + al - 1) // al * al
    for d in tot:
        SCRATCH["pk_" + d] = ("sbuf", [128, tot[d]], d)


_declare()


def _route(r, T, topo):
    s, d = T.cores[r], T.cores[(r + 3) % len(T.cores)]
    if topo.may_write(s, d):
        return s, None, d
    own = [c for c in topo.cores_of(s) if c not in T.cores and topo.may_write(c, d)]
    own.sort(key=lambda c: (topo.die(c) != topo.die(s), c))
    return s, own[0], d


def _mask(src, dst, topo):
    e = topo.engines(src, dst)[:8]
    return sum(1 << x for x in e), len(e)


def _send(g, T, topo, core, dst, src_ap, name, sem):
    rid, pid = topo.addr(dst, core)
    m, k = _mask(core, dst, topo)
    g.remote_dma(T[name][:], src_ap, T.sem[sem], T.sem["ls"], pid, rid, m)
    return k


def _relay(g, core, T, topo):
    for r in range(len(T.cores)):
        s, h, d = _route(r, T, topo)
        if h != core:
            continue
        tot = 0
        for t in range(1, NR_):
            for b in BAT:
                nm, sem = "i%s%d" % (b, t), "a%s%d" % (b, t)
                g.wait_ge(T.sem[sem], _mask(s, h, topo)[1])
                tot += _send(g, T, topo, core, d, T[nm][:], nm, sem)
        g.wait_ge(T.sem["ls"], tot)


def _weave(a, c, x0=0.0):
    L, k = [], 0
    for i, f in enumerate(a):
        L.append(f)
        want = int(max(((i + 1) / len(a) - x0) / (1.0 - x0), 0.0) * len(c) + 1e-6)
        L += c[k:want]
        k = max(k, want)
    return L + c[k:]


def _go(L):
    for f in L:
        f()


def rank_program(g, core, T, topo):
    rank = T.rank_of(core)
    if rank is None:
        return _relay(g, core, T, topo)
    MT, AT = (12, 18, 14, 22, 16), (10, 8, 9, 6, 8)
    eng = {"v": g.vector, "s": g.scalar, "t": g.tensor, "g": g, "y": g.sync}
    cnt, total, hist = {}, {}, {}
    known = {q: {} for q in eng}
    V, S, TE = g.vector, g.scalar, g.tensor

    def need(q, reads, writes):
        w = {}
        for keys, wr in ((reads, False), (writes, True)):
            for (key, c0, c1) in keys:
                for h in hist.get(key, ()):
                    if h[0] >= c1 or c0 >= h[1] or h[3] == q == "t":
                        continue
                    if not (wr or h[2] or (key[:2] == "ps" and h[3] != q)):
                        continue
                    s, n = h[4]
                    w[s] = max(w.get(s, 0), n)
        for s in w:
            if known[q].get(s, 0) < w[s]:
                eng[q].wait_ge(T.sem[s], w[s])
                known[q][s] = w[s]

    def note(q, reads, writes, ev):
        for keys, wr in ((reads, False), (writes, True)):
            for (key, c0, c1) in keys:
                L = hist.setdefault(key, [])
                if wr:
                    L[:] = [h for h in L if not (c0 <= h[0] and h[1] <= c1)]
                else:
                    L[:] = [h for h in L if h[2] or h[3] != q or not (c0 <= h[0] and h[1] <= c1)]
                L.append((c0, c1, wr, q, ev))

    def op(q, fn, reads, writes):
        need(q, reads, writes)
        sem = q + "c"
        total[sem] = cnt[q] = cnt.get(q, 0) + 1
        fn().then_inc(T.sem[sem], 1)
        note(q, reads, writes, (sem, cnt[q]))

    def dma(q, o, i, reads, writes, sem):
        need(q, reads, writes)
        eng[q].dma_start(o, i).then_inc(T.sem[sem], 16)
        total[sem] = 16
        note("dma" + sem, reads, writes, (sem, 16))

    def B(name, c0=0, c1=None, st=1):
        base, off, w = _POS[name] if name in _POS else (name, 0, SCRATCH[name][1][1])
        c1 = w if c1 is None else c1
        ap = T[base][:, off + c0:off + c1] if st == 1 else T[base][:, off + c0:off + c1:st]
        return ap, ((base, 0, 512) if base[:2] == "ps" else (base, off + c0, off + c1))

    def vcopy(o, i):
        op("v", lambda: V.tensor_copy(o[0], i[0]), [i[1]], [o[1]])

    def vgat(o, win, off):
        op("v", lambda: V.tensor_copy(o[0], win[0].indirect(off[0])), [win[1], off[1]], [o[1]])

    def sgat(o, win, off):
        op("s", lambda: S.activation(o[0], win[0].indirect(off[0]), F.Copy), [win[1], off[1]], [o[1]])

    def act(o, i, scale, bias, f=F.Copy):
        op("s", lambda: S.activation(o[0], i[0], f, bias=bias, scale=scale), [i[1]], [o[1]])

    def tt(o, a, b, f):
        op("v", lambda: V.tensor_tensor(o[0], a[0], b[0], f), [a[1], b[1]], [o[1]])

    def ttg(o, win, off, b, f):
        op("v", lambda: V.tensor_tensor(o[0], win[0].indirect(off[0]), b[0], f), [win[1], off[1], b[1]], [o[1]])

    def ts(o, a, s1, f1, s2=None, f2=None):
        rd = [a[1]] + [s[1] for s in (s1, s2) if isinstance(s, tuple)]
        x1 = s1[0] if isinstance(s1, tuple) else s1
        x2 = s2[0] if isinstance(s2, tuple) else s2
        if f2 is None:
            op("v", lambda: V.tensor_scalar(o[0], a[0], x1, None, f1), rd, [o[1]])
        else:
            op("v", lambda: V.tensor_scalar(o[0], a[0], x1, x2, f1, f2), rd, [o[1]])

    def lin(b, o, i, scale, bias):
        if b == "B":
            act(o, i, scale, bias)
        else:
            ts(o, i, scale, A_.mult, bias, A_.add)

    def red(o, a, f):
        op("v", lambda: V.tensor_reduce(o[0], a[0], X_, f), [a[1]], [o[1]])

    def ms(o, c):
        op("v", lambda: V.memset(o[0], c), [], [o[1]])

    def mm(o, l, r, st, sp):
        op("t", lambda: TE.matmul(o[0], l[0], r[0], st, sp), [l[1], r[1]], [o[1]])

    def iota(o, pat, base, ch, whole=False):
        if whole:
            op("g", lambda: g.iota(o[0], pat, base, ch), [], [o[1]])
        else:
            op("g", lambda: g.iota(o[0], pat, base, ch, allow_small_or_imprecise_dtypes=True), [], [o[1]])

    def asel(o, i, pat, f, base, ch):
        op("g", lambda: g.affine_select(o[0], i[0], pat, f, 0.0, base, ch), [i[1]], [o[1]])

    for q, nm, c1, src, sem in (("s", "GEN", 1024, T.gen, "ld3"), ("y", "XC", 64, T.cla, "ld0"), ("y", "XD", 64, T.par, "ld1"),
                                ("y", "XL", 4, T.lit, "ld2"), ("y", "VAL", 2048, T.val, "ld4")):
        o = B(nm, 0, c1)
        dma(q, o[0], src[:], [], [o[1]], sem)

    iota(B("PI", 0, 1), [[1, 1]], 0, 1, True)
    ms(B("ONE"), 1.0)
    asel(B("B1"), B("ONE"), [[-16, 8], [0, 16]], A_.is_ge, 0, 1)
    asel(B("BO"), B("B1"), [[16, 8], [0, 16]], A_.is_ge, 15, -1)
    asel(B("IDN"), B("ONE"), [[-1, 128]], A_.is_equal, 0, 1)
    asel(B("E0"), B("ONE"), [[0, 128]], A_.is_equal, 0, 1)
    iota(B("JT"), [[0, 32], [1, 16]], 0, 0)
    iota(B("A16"), [[16, 32], [0, 16]], 0, 0)
    iota(B("CW0"), [[240, 64]], 0, 0, True)
    iota(B("B64"), [[1, 64]], 0, 0)
    iota(B("PENC"), [[2, 64]], 2048, 0)
    ms(B("VAL", 2048, 2176), 0.0)
    ts(B("PI", 1, 2), B("PI", 0, 1), 15, A_.bitwise_and)
    ts(B("PI", 2, 3), B("PI", 0, 1), 16, A_.bitwise_and)
    ms(B("DC", 0, 32), 32.0)
    vcopy(B("PC", 0, 1), B("PI", 1, 2))
    ts(B("PC", 1, 2), B("PI", 2, 3), 0.0, A_.is_equal)
    ts(B("PC", 2, 3), B("PI", 2, 3), 16.0, A_.is_equal)
    ts(B("PC", 3, 4), B("PC", 0, 1), 16.0, A_.mult)
    for q in range(4):
        ts(B("PC", 4 + q, 5 + q), B("PC", 0, 1), 16.0 * q, A_.add)
    for q in range(4):
        ts(B("PC", 8 + q, 9 + q), B("PC", 4 + q, 5 + q), 2.0, A_.mult, 2048.0, A_.add)
    for p in (0, 1):
        op("v", lambda p=p: V.memset(T["SB%d" % p][:, 0, :], 0.0), [], [("SB%d.%d" % (p, j), 0, 1) for j in range(16)])
    ms(B("DC", 32, 64), -32.0)
    ms(B("THR", 2, 3), -1024000.0 * (AT[0] - 1) - 500.0)
    ms(B("THR", 3, 4), 1024000.0 * (AT[0] - 1) + 500.0)
    ms(B("MSK"), 1.0)
    ms(B("MKK"), 1.0)

    def flip(q_, Z, ZT, src, dst):
        def blocks():
            for q in range(4):
                for h in range(2):
                    o, i, m = B(Z, 32 * q + 16 * h, 32 * q + 16 * h + 16), src(q), B("PC", 1 + h, 2 + h)
                    if q_ == "s":
                        op("s", lambda: S.activation(o[0], i[0], F.Copy, scale=m[0]), [i[1], m[1]], [o[1]])
                    else:
                        ts(o, i, m, A_.mult)

        def turn():
            a, b = B(Z), B(ZT)
            op("v", lambda: V.transpose(b[0], a[0]), [a[1]], [b[1]])
        return [blocks, turn] + [lambda q=q: tt(dst(q), B(ZT, 32 * q, 32 * q + 16), B(ZT, 32 * q + 16, 32 * q + 32), A_.add)
                                 for q in range(4)]

    def lane16(pre, t, part):
        def f(q):
            b = "A" if 16 * q < BAT["B"][0] else "B"
            c = part * BAT[b][1] + 16 * q - BAT[b][0]
            return B("%s%s%d" % (pre, b, t), c, c + 16)
        return f

    vcopy(B("FX"), B("XC"))
    fc = flip("s", "Z", "ZT", lambda q: B("FX", q, 64, 4), lane16("i", 0, 0))
    fd = flip("v", "Z2", "ZT2", lambda q: B("FX2", q, 64, 4), lane16("i", 0, 1))
    fc[0]()
    vcopy(B("FX2"), B("XD"))
    HF = ((0, 512), (512, 1024))
    for c0, c1 in HF:
        vcopy(B("PT", 2 * c0, 2 * c1, 2), B("GEN", c0, c1))
    for i, (c0, c1) in enumerate(HF):
        act(B("PM", c0, c1), B("PT", 2 * c0, 2 * c1, 2), 0.49994, MAGIC)
        act(B("psD%d" % i), B("PM", c0, c1), 4.0, -4.0 * MAGIC)
    _go(fc[1:2])
    ts(B("GM", 0, 512), B("GEN", 0, 512), 1.0, A_.subtract)
    _go(fc[2:])
    ts(B("GM", 512, 1024), B("GEN", 512, 1024), 1.0, A_.subtract)
    _go(fd)
    ts(B("LT0"), B("XL"), 1, A_.bitwise_and)
    for b in BAT:
        a0, n = BAT[b]
        vcopy(B("i%s0" % b, 2 * n, 2 * n + n // 16), B("XL", a0 // 16, (a0 + n) // 16))
    ts(B("LT1"), B("LT0"), -2.0, A_.mult, 1.0, A_.add)
    tt(B("PT", 1, 1024, 2), B("psD0"), B("GM", 0, 512), A_.subtract)
    for b in BAT:
        a0, n = BAT[b]
        q0, nq = a0 // 16, n // 16
        tt(B("i%s0" % b, 2 * n + nq, 2 * n + 2 * nq), B("XL", q0, q0 + nq), B("LT1", q0, q0 + nq), A_.add)
    tt(B("PT", 1025, 2048, 2), B("psD1"), B("GM", 512, 1024), A_.subtract)

    def late_constants():
        ms(B("SL0"), 1.0)
        asel(B("SL0"), B("SL0"), [[1, 16], [0, 8], [-1, 16]], A_.is_equal, 0, 0)
        asel(B("SL0"), B("SL0"), [[0, 16], [-16, 8], [0, 16]], A_.is_ge, 0, 1)
        asel(B("SL0"), B("SL0"), [[0, 16], [16, 8], [0, 16]], A_.is_ge, 15, -1)
        ms(B("MSK", 15, 256, 16), -1.0)
        ms(B("MKK", 0, 512, 16), 0.0)
        ts(B("BOV"), B("BO"), -1024.0, A_.mult)
        ts(B("BOS"), B("BO"), -16.0, A_.mult)
        vcopy(B("BOH"), B("BO"))
        vcopy(B("IDH"), B("IDN"))
        ts(B("OHT"), B("JT"), B("PC", 0, 1), A_.is_equal)
        ts(B("CW"), B("CW0"), B("PC", 3, 4), A_.add)
        for q, c0, w in ((0, 0, 32), (1, 32, 32), (2, 64, 64), (3, 128, 64)):
            ts(B("LMT", c0, c0 + w), B("B64", 0, w), B("PC", 4 + q, 5 + q), A_.is_lt, B("PC", 8 + q, 9 + q), A_.mult)

    def step1(t, b):
        a0, n = BAT[b]
        nq = n // 16
        I, O = "i%s%d" % (b, t), "o%s%d" % (b, t)
        return [
            lambda: vcopy(B("LL" + b), B(I, 2 * n, 2 * n + 2 * nq)),
            lambda: vgat(B("XV" + b), B("VAL", 0, 2048), B("LL" + b)),
            lambda: tt(B("LE" + b), B("XV" + b, 0, n), B("XV" + b, n, 2 * n), A_.is_lt),
            lambda: mm(B("psR", 0, n), B("BO"), B("LE" + b), True, True),
            lambda: tt(B("DMC" + b), B(I, n, 2 * n), B(I, 0, n), A_.subtract),
            lambda: ts(B("FL" + b), B("psR", 0, n), 8.5, A_.is_ge),
            lambda: tt(B("T2" + b), B("FL" + b), B("DMC" + b), A_.mult),
            lambda: tt(B(O, n, 2 * n), B("T2" + b), B(I, 0, n), A_.add),
            lambda: vcopy(B("CU" + b), B(O, n, 2 * n)),
        ]

    def image(b, x0, x1):
        a0 = BAT[b][0]
        vgat(B("IMG", 16 * x0, 16 * x1), B("PT"), B("CU" + b, x0 - a0, x1 - a0))

    def imf(b):
        a0, n = BAT[b]
        if b == "A":
            vcopy(B("IFA"), B("IMG", 16 * a0, 16 * (a0 + n)))
        else:
            sgat(B("IFB"), B("PT"), B("CU" + b))

    def values(f, x0, x1):
        f(B("W", 256 * x0, 256 * x1), B("VAL", 0, 2048), B("IMG", 16 * x0, 16 * x1))

    def scans(c):
        p = c & 1
        sb, yb = T["SB%d" % p], T["YB%d" % p]
        wr = ("W", 4096 * c, 4096 * (c + 1))

        def one(j):
            op("v", lambda: V.tensor_tensor_scan(sb[:, 1:257, j], T.W[:, 4096 * c + j:4096 * (c + 1):16], T.MSK[:], 0.0, A_.max, A_.mult),
               [wr, ("MSK", 0, 256)], [("SB%d.%d" % (p, j), 1, 257)])

        def two(j):
            op("v", lambda: V.tensor_tensor_scan(yb[:, :, j], T.W[:, 4096 * c + j:4096 * (c + 1):16], sb[:, 0:256, j], 0.0, A_.max, A_.min),
               [wr, ("SB%d.%d" % (p, j), 0, 256)], [("YB%d.%d" % (p, j), 0, 256)])
        out = [lambda: one(0)]
        for j in range(1, 16):
            out.append(lambda j=j: one(j))
            out.append(lambda j=j: two(j - 1))
        out.append(lambda: two(15))
        return out

    def diff(c):
        p = c & 1
        o = B("psD%d" % p, 0, 256)
        op("t", lambda: TE.matmul(o[0], T.IDN[:], T["SB%d" % p][:, 16:257:16, :], True, False),
           [("IDN", 0, 128)] + [("SB%d.%d" % (p, j), 16, 257) for j in range(16)], [o[1]])
        op("t", lambda: TE.matmul(o[0], T.IDN[:], T["YB%d" % p][:, 15:256:16, :], False, True),
           [("IDN", 0, 128)] + [("YB%d.%d" % (p, j), 15, 256) for j in range(16)], [o[1]])

    def unit(t, c, q):
        i, o = B("psD%d" % (c & 1), 0, 256), B("U", 256 * c, 256 * c + 256)
        if q == "v":
            ts(o, i, -float(MT[t]), A_.is_lt)
        else:
            act(o, i, -1000.0, -1000.0 * (MT[t] + 0.5), F.Sigmoid)

    def votes(c):
        o, c0 = B("psV%d" % (c & 1), 0, 256), 256 * (c % 2)
        mm(o, B("E0"), B("A16", c0, c0 + 256), True, False)
        mm(o, B("E0"), B("JT", 0, 256), False, False)
        mm(o, B("BOV"), B("U", 256 * c, 256 * c + 256), False, True)

    def scanmin(o, i):
        n = o[1][2] - o[1][1]
        m = B("MKK", 0, n)
        op("v", lambda: V.tensor_tensor_scan(o[0], m[0], i[0], 0.0, A_.mult, A_.min), [m[1], i[1]], [o[1]])

    def best(c):
        scanmin(B("K1", 256 * c, 256 * c + 256), B("psV%d" % (c & 1), 0, 256))

    def post(t, b, x0, x1):
        a0, n = BAT[b]
        nq, e0, e1, w, m0 = n // 16, 16 * a0, 16 * (a0 + n), a0 + n, 2 * a0
        I, O = "i%s%d" % (b, t), "o%s%d" % (b, t)
        km = lambda: B("K1", e0 + 15, e1, 16)

        def promoted():
            for o, f, c in (("PRO", -1000.0, 2), ("NP", 1000.0, 3)):
                x, y, z = B(o, a0, a0 + n), km(), B("THR", c, c + 1)
                op("s", lambda: S.activation(x[0], y[0], F.Sigmoid, bias=z[0], scale=f), [y[1], z[1]], [x[1]])

        def newc():
            for k in range(16):
                mm(B("psN", 0, n), B("SEL", 128 * k, 128 * k + 128), B("MK", e0 + k, e1, 16), k == 0, k == 15)

        def sums():
            mm(B("psS"), B("E0"), B("JT"), True, False)
            mm(B("psS"), B("BOS"), B("PR", e0, e1), False, True)

        def marks():
            mm(B("psR", 0, n), B("IDH"), B("PEN" + b), True, False)
            mm(B("psR", 0, n), B("BOH"), B("XX" + b), False, True)

        def put():
            x, e, z = B("VAL"), B("EL" + b), B("ZE" + b)
            op("v", lambda: V.tensor_copy(x[0].indirect(e[0]), z[0]), [e[1], z[1]], [x[1]])
        L = [
            lambda: vcopy(B("KI" + b), km()),
            lambda: ts(B("QI" + b), B("KI" + b), 1023, A_.bitwise_and),
            lambda: vcopy(B("LU" + b), B("QI" + b)),
            lambda: sgat(B("UX", e0, e1), B("U", e0, e1), B("LU" + b)),
            lambda: tt(B("WI" + b), B("QI" + b), B("CW", 0, n), A_.add),
            promoted,
            lambda: vcopy(B("LW" + b), B("WI" + b)),
            lambda: ttg(B("MK", e0, e1), B("OHT"), B("LU" + b), B("IF" + b), A_.mult),
            newc,
            lambda: ttg(B("PR", e0, e1), B("W", 16 * e0, 16 * e1), B("LW" + b), B("UX", e0, e1), A_.mult),
            sums,
            lambda: tt(B("PEN" + b), B("NP", a0, a0 + n), B("PENC", a0, a0 + n), A_.mult),
            lambda: tt(B("DN" + b), B(I, n, 2 * n), B("NP", a0, a0 + n), A_.mult),
            lambda: tt(B("NCG" + b), B("psN", 0, n), B("PRO", a0, a0 + n), A_.mult),
            lambda: tt(B(O, 0, n), B("NCG" + b), B("DN" + b), A_.add),
        ]
        M = [
            lambda: scanmin(B("K2", e0, e1), B("psS")),
            lambda: vcopy(B("K2I" + b), B("K2", e0 + 15, e1, 16)),
            lambda: ts(B("KR" + b), B("K2I" + b), 15, A_.bitwise_and),
            lambda: ts(B("OHK" + b), B("KR" + b), B("PC", 0, 1), A_.is_equal),
            lambda: tt(B("XX" + b), B("OHK" + b), B("NCG" + b), A_.mult),
            marks,
            lambda: tt(B("DM" + b), B("psR", 0, n), B("OHT", 0, n), A_.mult),
            lambda: lin(b, B("PREP", a0, a0 + n), B("psR", 0, n), 0.49994, MAGIC),
        ]
        M += [lambda q=q: red(B("NL" + b, q, q + 1), B("DM" + b, 16 * q, 16 * q + 16), A_.add) for q in range(nq)]
        M += [
            lambda: ts(B("PCL" + b), B("NL" + b, 0, nq), 0.49994, A_.mult, MAGIC, A_.add),
            lambda: lin(b, B("NM" + b), B("NL" + b, 0, nq), -1.0, 1.0),
        ]
        M += [lambda q=q: ts(B("EQ" + b, w * q, w * q + w), B("PREP", 0, w), B("PCL" + b, q, q + 1), A_.is_equal) for q in range(nq)]
        M += [lambda: lin(b, B("FP" + b), B("PCL" + b), 4.0, -4.0 * MAGIC)]
        N = [
            lambda: tt(B("EM" + b, 0, nq * w), B("EQ" + b, 0, nq * w), B("LMT", m0, m0 + nq * w), A_.mult),
            lambda: tt(B("NL" + b, nq, 2 * nq), B("FP" + b), B("NM" + b), A_.add),
        ]
        N += [lambda q=q: red(B("DV" + b, q, q + 1), B("EM" + b, w * q, w * q + w), A_.max) for q in range(nq)]
        N += [
            lambda: ts(B("DV" + b, nq, 2 * nq), B("DV" + b, 0, nq), 1.0 + 2.0 ** -11, A_.mult),
            lambda: tt(B("OL" + b), B("NL" + b), B("DV" + b), A_.max),
            lambda: vcopy(B("EL" + b), B("OL" + b)),
        ]
        E = [
            lambda: ttg(B("YE" + b), B("VAL"), B("EL" + b), B("DC"), A_.add),
            lambda: ts(B("ZE" + b), B("YE" + b), 255.0, A_.min, 0.0, A_.max),
            put,
        ]
        return L + _weave(M, x0) + N[:2] + _weave(N[2:], x1), E

    def newmarks(t, b):
        n = BAT[b][1]
        I, O = "i%s%d" % (b, t), "o%s%d" % (b, t)
        old = lambda: B(I, 2 * n, 2 * n + n // 8)
        return [
            lambda: ts(B("KP" + b), B("NL" + b), 2047.5, A_.is_lt),
            lambda: tt(B("DL" + b), B("NL" + b), old(), A_.subtract),
            lambda: tt(B("DK" + b), B("DL" + b), B("KP" + b), A_.mult),
            lambda: tt(B(O, 2 * n, 2 * n + n // 8), B("DK" + b), old(), A_.add),
        ]

    def parity(t):
        return [
            lambda: red(B("THR", 1, 2), B("PRO"), A_.add),
            lambda: vcopy(B("TI", 0, 1), B("THR", 1, 2)),
            lambda: ts(B("TI", 1, 2), B("TI", 0, 1), 1, A_.bitwise_and),
            lambda: ts(B("THR", 2, 3), B("TI", 1, 2), -1024000.0, A_.mult, -1024000.0 * (AT[t] - 1) - 500.0, A_.add),
            lambda: ts(B("THR", 3, 4), B("TI", 1, 2), 1024000.0, A_.mult, 1024000.0 * (AT[t] - 1) + 500.0, A_.add),
        ]

    src, hand, dst = _route(rank, T, topo)
    sent = [0]

    def send(t, b):
        if t == NR_ - 1:
            return
        o = B("o%s%d" % (b, t))
        need("g", [o[1]], [])
        to = hand if hand is not None else dst
        sent[0] += _send(g, T, topo, core, to, o[0], "i%s%d" % (b, t + 1), "a%s%d" % (b, t + 1))

    into = _route((rank - 3) % len(T.cores), T, topo)
    arr = _mask(into[1] if into[1] is not None else into[0], core, topo)[1]

    def arrive(t):
        for b in BAT:
            i, sem = B("i%s%d" % (b, t)), "a%s%d" % (b, t)
            total[sem] = arr
            note("rem" + sem, [], [i[1]], (sem, arr))

    def store(q, y, nm, sem, c1):
        o = B(nm, 0, c1)
        dma(q, y[:], o[0], [o[1]], [], sem)

    def outputs(q, part, fx, z, zt, y, yd, sem):
        t = NR_ - 1
        L = [lambda b=b: vcopy(B(fx, BAT[b][0], sum(BAT[b])), B("o%s%d" % (b, t), part * BAT[b][1], (part + 1) * BAT[b][1])) for b in BAT]
        return L + flip("s", z, zt, lambda x: B(fx, 16 * x, 16 * x + 16), lambda x: B(y, x, 64, 4)) + [lambda: store(q, yd, y, sem, 64)]

    for t in range(NR_):
        last = t == NR_ - 1
        if t:
            arrive(t)
        _go(step1(t, "A"))
        image("A", 0, 16)
        values(sgat, 0, 16 - NV)
        image("A", 16, 32)
        if t == 0:
            late_constants()
        values(vgat, 16 - NV, 16)
        values(sgat, 16, 32)
        imf("A")
        _go(_weave(scans(0), (parity(t) if t else []) + step1(t, "B") + [lambda: image("B", 32, 48)], 0.3))
        values(sgat, 32, 40)
        diff(0)
        unit(t, 0, "s")
        votes(0)
        values(sgat, 40, 48)
        _go(_weave(scans(1), [lambda: image("B", 48, 64), lambda: best(0)], 0.1))
        diff(1)
        unit(t, 1, "v")
        votes(1)
        if t == 0:
            vcopy(B("SEL"), B("SL0"))
        best(1)
        chain, late = post(t, "A", [], newmarks(t, "A"))
        _go(chain[:6])
        values(sgat, 48, 64)
        imf("B")
        _go(chain[6:PRE])
        _go(_weave(scans(2), chain[PRE:] + [lambda: send(t, "A")]))
        diff(2)
        unit(t, 2, "s")
        votes(2)
        _go(_weave(scans(3), [lambda: best(2)], 0.2))
        diff(3)
        late[0]()
        unit(t, 3, "v")
        votes(3)
        _go(late[1:])
        best(3)
        x0 = outputs("s", 1, "FX2", "Z2", "ZT2", "YD", T.yd, "st2") + outputs("y", 0, "FX", "Z", "ZT", "YC", T.yc, "st1") if last else []
        chain, late = post(t, "B", x0, newmarks(t, "B"))
        _go(chain)
        send(t, "B")
        _go(late)

    store("y", T.yv, "VAL", "st0", 2048)
    for b in BAT:
        a0, n = BAT[b]
        vcopy(B("YL", a0 // 16, (a0 + n) // 16), B("o%s%d" % (b, NR_ - 1), 2 * n, 2 * n + n // 16))
    store("s", T.yl, "YL", "st3", 4)
    total["ls"] = sent[0]
    for s in total:
        if total[s]:
            g.wait_ge(T.sem[s], total[s])
